import numpy as np, ml_dtypes
CORES = [5,29,101,125,133,157,229,253]
N = 8
BF = ml_dtypes.bfloat16
C, I, P, T, ST = 2048, 256, 512, 3, 1
SX, SP = 8, 2
def parts(rng):
    return rng.integers(0, 256, (N, 8, C, 16)), rng.integers(0, 4096, (N, 8, I, 16)), rng.integers(0, 4096, (N, 8, P, 16)), rng.integers(1, 256, (N, 8, 16))
def turn(a):
    return np.ascontiguousarray(np.swapaxes(a, 2, 3)).reshape(N, 128, -1)
def pack(x, w, p, t):
    return {"xt": turn(x).astype(np.float32).astype(BF), "wd": turn(w).astype(np.int32), "pd": turn(p).astype(np.int32), "wt": np.reshape(t, (N, 128, 1)).astype(np.int32)}
def place(a, b, s):
    return ((a * b >> 5) + 37 * a + b + s) & (C - 1)
def setup_inputs(rng):
    x, w, p, t = parts(rng)
    return pack(x, w, p, t)
def setup_inputs_spread(rng):
    x, w, p, t = parts(rng)
    s = rng.choice(np.array([0.0, 0.25, 0.5, 1.0]), (N, 8, 1, 1))
    x = (x * np.exp2(-8 * s * rng.random((N, 8, C, 1)))).astype(np.int64)
    w = np.where(rng.random((N, 8, I, 1)) < 0.5, np.exp2(12 * rng.random(w.shape)).astype(np.int64) - 1, w)
    p = np.where(rng.random((N, 8, P, 1)) < 0.5, np.exp2(12 * rng.random(p.shape)).astype(np.int64) - 1, p)
    t = np.minimum(np.exp2(8 * rng.random(t.shape)).astype(np.int64), 255)
    return pack(x, np.minimum(w, 4095), np.minimum(p, 4095), t)
def setup_inputs_ends(rng):
    x, w, p, t = parts(rng); m = np.arange(16); s = np.arange(32)
    x = np.where(x < 128, 0, 255); x = np.where(rng.random(x.shape) < 0.1, np.abs(x - 1), x)
    x[:, :, (s - 1) & (C - 1)] = 0; x[:, :, (s + 37 * 4095) & (C - 1)] = 255
    w = np.where(rng.random((N, 8, I, 1)) < 0.75, 4095 * rng.integers(0, 2, w.shape), w)
    kind = rng.integers(0, 4, (N, 8, P, 1))
    p = np.where(kind == 0, 0, np.where(kind == 1, 4095, np.where(kind == 2, 4095 * rng.integers(0, 2, p.shape), p)))
    v = rng.integers(64, 2000, (N, 8))
    w[:, :, I - 1] = 0; w[:, :, I - 1, 14] = v; w[:, :, I - 1, 15] = 4095
    w[:, :, I - 2] = 4095; w[:, :, I - 2, 0] = 0; w[:, :, I - 2, 1] = v
    w[:, :, 0] = 0; w[:, :, 0, 15] = 4095; w[:, :, 1] = 4095 * (m % 2)
    p[:, :, 0] = 4095; p[:, 1::2, 0, 15] = 0
    t = np.where(t < 128, 1, 255); t[:, 0] = 1; t[:, 7] = 255
    return pack(x, w, p, t)
def setup_inputs_corners(rng):
    x, w, p, t = parts(rng); m = np.arange(16)
    kw = rng.integers(0, 6, (N, 8, I, 1)); z = rng.integers(0, 16, (N, 8, I, 1)); one = w[..., :1]
    w = np.where(kw == 0, one, np.where(kw == 1, w[..., m % 2], np.where(kw == 2, (one & 1023) + 1024 * (w & 3), np.where(kw == 3, np.where(m == z, w[..., 1:2], one), np.where(kw == 4, w[..., m % 8], w)))))
    kp = rng.integers(0, 4, (N, 8, P, 1))
    p = np.where(kp == 0, p[..., :1], np.where(kp == 1, p[..., m % 4], np.where(kp == 2, 4095 * (p & 1), p)))
    p[:, 1::2, ::SP] = w[:, 1::2]
    x[:, 0::4] = x[:, 0::4] & 1; x[:, 1::4] = x[:, 1::4][:, :, (np.arange(C) >> 2) & 7]; x[:, 2::4] = 255 * (x[:, 2::4] & 1)
    t[:, 0] = 1; t[:, 1] = 255; t[:, 2] = np.where(m == 15, 255, 1); t[:, 3] = np.where(m == 0, 1, 255)
    return pack(x, w, p, t)
def setup_inputs_crowd(rng):
    x, w, p, t = parts(rng); g1 = int(rng.integers(0, 8))
    for q in (0, 1, N - 1):
        for g in range(8):
            but = (g == g1) if q == 1 else (q > 1 and rng.random() < 0.5)
            base = rng.integers(0, 256, 16); x[q, g] = base
            if but:
                a = w[q, g]; b = np.roll(a, -1, axis=1)
                n = np.bincount(np.concatenate([place(a, b, 0).ravel(), place(b, a, 0).ravel()]), minlength=C)
                x[q, g, int(rng.choice(np.flatnonzero(n == 1)))] = 255 - base
    al = np.argsort(rng.random((8, 4096)), axis=1)[:, :4]
    a = np.take_along_axis(al, rng.integers(0, 4, (8, I)), 1)[:, :, None]; b = (a + rng.integers(1, C // 4, (8, I, 1))) & 4095
    w[2] = np.where(np.arange(16) == rng.integers(0, 16, (8, I, 1)), b, a)
    p[2, :, :, :4] = al[:, None, :]; p[2] = np.take_along_axis(p[2], np.argsort(rng.random((8, P, 16)), axis=2), 2)
    return pack(x, w, p, t)
def setup_inputs_brink(rng):
    x, w, p, t = parts(rng); m = np.arange(16)
    for q in range(N):
        for g in range(8):
            s = 1 + rng.permutation(36)
            cut = np.zeros(36, np.int64); cut[8:12] = 1
            if g % 2 == 0:
                cut[12:] = rng.integers(2, 256, 24); cut[35] = 255
            else:
                cut[12:24] = 2040; cut[24:] = 2041
            o = np.argsort(rng.random((36, 16)), axis=1)
            far = 255 - np.clip(cut[:, None] - 255 * o, 0, 255)
            lo = (255 - far) * rng.integers(0, 2, (36, 16)); up = rng.random((36, 16)) < 0.5
            x[q, g, s] = np.where(up, lo + far, lo); x[q, g, 37 * s] = np.where(up, lo, lo + far)
            p[q, g] = s[rng.integers(0, np.where(rng.random((P, 1)) < 0.5, 24, 36), (P, 16))]
            z1 = rng.integers(1, 7, (I, 1)); z2 = z1 + 2 + rng.integers(0, 8, (I, 1))
            v = np.where(m == z1, s[rng.integers(8, 12, (I, 1))], np.where(m == z2, s[rng.integers(0, 8, (I, 1))], 0))
            w[q, g] = np.where(rng.random((I, 1)) < 0.75, v, w[q, g])
    return pack(x, w, p, t)
def check_inputs(d):
    bad = []
    for k, lo, hi in (("xt", 0, 255), ("wd", 0, 4095), ("pd", 0, 4095), ("wt", 1, 255)):
        a = np.asarray(d[k]).astype(np.float64)
        if not (np.all(a >= lo) and np.all(a <= hi) and np.all(a == np.floor(a))): bad.append("range of " + k)
    return bad
def reference(xt, wd, pd, wt):
    x = np.ascontiguousarray(np.swapaxes(xt.astype(np.float32).astype(np.int32).reshape(N, 8, 16, C), 2, 3))
    w = np.ascontiguousarray(np.swapaxes(wd.astype(np.int64).reshape(N, 8, 16, I), 2, 3))
    p = np.ascontiguousarray(np.swapaxes(pd.astype(np.int64).reshape(N, 8, 16, P), 2, 3))
    wts = wt.astype(np.int64).reshape(N, 8, 1, 16)
    gi = np.arange(8)[:, None]; ti = np.arange(I)[None, :]; g3 = np.arange(8)[:, None, None]
    A = np.zeros(N, np.int64)
    for t in range(T):
        A2 = np.zeros(N, np.int64)
        for r in range(N):
            q = (r + ST * t) % N
            v = w[r].copy(); v1 = np.roll(v, -1, axis=2)
            f = x[q][g3, place(v, v1, A[q])]; h = x[q][g3, place(v1, v, A[q])]
            e = np.add.reduce(np.abs(f - h), axis=3)
            k = np.argmax(e, axis=2); kn = (k + 1) & 15
            c = np.where(e[gi, ti, (k - 1) & 15] >= e[gi, ti, kn], k, kn)
            u = np.add.reduce(wts[q] * f[gi, ti, k], axis=2)
            b = p[q][gi, u & (P - 1)]
            before = v[gi, ti, (c - 1) & 15][:, :, None]; after = v[gi, ti, (c + 1) & 15][:, :, None]
            y = x[q][g3, place(before, b, A[q])]; z = x[q][g3, place(b, after, A[q])]
            E = np.add.reduce(np.abs(y - z), axis=3)
            j = np.argmin(E, axis=2)
            good = 2 * E[gi, ti, j] < e[gi, ti, k]
            mend = v.copy(); mend[gi, ti, c] = b[gi, ti, j]
            swap = v.copy(); swap[gi, ti, k] = v[gi, ti, kn]; swap[gi, ti, kn] = v[gi, ti, k]
            new = np.where(good[:, :, None], mend, swap)
            gg, ii = np.nonzero(good)
            p[q, gg, SP * ii + (u[gg, ii] & (SP - 1))] = new[gg, ii]
            x[q, gi, SX * ti + (u & (SX - 1))] = (y[gi, ti, j] + z[gi, ti, j]) >> 1
            w[r] = new; A2[q] = (8 * I - len(gg)) & 31
        A = A2
    return {"yw": turn(w).astype(np.float32), "yp": turn(p).astype(np.float32), "yx": turn(x).astype(np.float32).astype(BF)}

@@ -1,0 +1,614 @@
+from concourse.mybir import AluOpType as A, ActivationFunctionType as F, AxisListType as X
+
+NV = 3
+NH = 2
+CW = 256 // NH
+NC = CW // 16
+NS = 4
+NP = 2
+SW = CW // NS
+EXP = False
+M5 = 1.5 * 2.0 ** 28
+
+f32, bf, f16, i32, u16 = "float32", "bfloat16", "float16", "int32", "uint16"
+SCRATCH = {
+    "wi": ("sbuf", [128, 256], i32), "pi": ("sbuf", [128, 512], i32), "wti": ("sbuf", [128, 4], i32),
+    "xa": ("sbuf", [128, 2080], bf), "xb": ("sbuf", [128, 2080], bf),
+    "sw": ("sbuf", [128, 768], f32), "op": ("sbuf", [128, 512], f32), "wn": ("sbuf", [128, 512], f32),
+    "ia": ("sbuf", [128, 128], i32), "ib": ("sbuf", [128, 128], i32), "ic": ("sbuf", [128, 160], i32),
+    "idd": ("sbuf", [128, 128], i32), "ie": ("sbuf", [128, 16], i32), "ig": ("sbuf", [128, 128], i32),
+    "rr": ("sbuf", [128, 128], f32),
+    "one32": ("sbuf", [128, 128], f32), "oneb": ("sbuf", [128, 128], bf), "c8k": ("sbuf", [128, 128], bf),
+    "i32m": ("sbuf", [128, 128], f32), "sw32": ("sbuf", [128, 128], f32),
+    "mats": ("sbuf", [128, 24 * 128], bf), "rm": ("sbuf", [128, 16 if EXP else 16 * 128], bf),
+    "eb": ("sbuf", [128, 160], bf), "en": ("sbuf", [128, 160], bf), "ep": ("sbuf", [128, 160], bf),
+    "ew": ("sbuf", [128, 160], bf), "dbig": ("sbuf", [128, 160], bf),
+    "ck": ("sbuf", [128, CW], f32), "cke": ("sbuf", [128, CW], f32),
+    "cz": ("sbuf", [128, CW], f16), "coh": ("sbuf", [128, 4 * CW], bf), "cac": ("sbuf", [128, 2 * CW], bf),
+    "msk": ("sbuf", [128, CW], f32), "dia": ("sbuf", [128, CW], bf), "cols": ("sbuf", [128, 32], f32),
+    "ti": ("sbuf", [128, 16], f32), "b16": ("sbuf", [128, 16], f32), "ct": ("sbuf", [128, 16], f32),
+    "cb": ("sbuf", [128, 32], f32), "lsb": ("sbuf", [128, 16], f32), "t256": ("sbuf", [128, 16], f32),
+    "gd": ("sbuf", [128, 32], bf), "acol": ("sbuf", [128, 16], f32),
+    "ui": ("sbuf", [128, 16], i32), "sm": ("sbuf", [128, 32], i32), "sm2": ("sbuf", [128, 32], f32),
+    "lx": ("sbuf", [128, 16], u16), "g6": ("sbuf", [128, 16], f32), "ls": ("sbuf", [128, 16], u16),
+    "lc": ("sbuf", [128, 16], u16),
+    "w16": ("sbuf", [128, NV * 256], f16),
+    "wo": ("sbuf", [128, (NV - 1) * 256], f16),
+}
+for _h in range(NH):
+    for _n, _w, _d in (("p32", 2 * CW, f32), ("dw", CW, f32), ("xi", 2 * CW, i32), ("off", 2 * CW, u16),
+                       ("fb", 16 * CW, bf), ("db", 16 * CW, bf), ("rs", CW, i32), ("ix", 16, i32),
+                       ("lk", 16, u16), ("kb", CW, f16), ("th", 16, f32), ("gg", 2 * CW, bf), ("fk", CW, bf),
+                       ("u9", 16, i32), ("lb", 16, u16), ("b32", CW, f32), ("tt", 2 * CW, f16), ("s32", CW, f32),
+                       ("ohp", CW, bf), ("g7", 16, f32), ("lg", 16, u16), ("bj", CW, f16), ("tm", CW, f32),
+                       ("hf", CW, f32), ("av", CW, i32), ("wf", CW, f32), ("lf", CW, f32)):
+        SCRATCH["%s%d" % (_n, _h)] = ("sbuf", [128, _w], _d)
+    SCRATCH["ab%d" % _h] = ("sbuf", [128, NC, 16, 16], bf)
+    for _b in range(4):
+        SCRATCH["ps%d%d" % (_h, _b)] = ("psum", [128, 512], f32)
+
+SEMAPHORES = (["cv", "cs", "cp", "cg", "sent"] + ["d%d" % k for k in range(16)]
+              + ["arr%d%d" % (t, h) for t in range(NV) for h in range(NH)]
+              + ["hop%d%d" % (t, h) for t in range(NV - 1) for h in range(NH)])
+
+PAR = {"g": 1.605, "s": 2.916, "pe": 0.569, "lat": 100.0, "far": 5700.0}
+KEYS = {"a0": -2.58, "g00": -2.41, "m0": 0.74, "a1": -0.03, "g01": 8.71, "m1": 3.7, "g10": 3.72, "e0": 9.16, "g11": 11.94, "e1": 8.51, "z0": 12.27}
+FV = set([(0, 0, 0, 1), (1, 0, 1, 2), (0, 1, 0, 1), (2, 0, 0, 1), (2, 0, 1, 2), (2, 1, 0, 1), (2, 1, 1, 2), (1, 0, 0, 1), (1, 1, 0, 1)])
+AHEAD = 0.002
+SOON = [450.0, 0.1]
+JIT = (792, 0.003)
+PLAN = {}
+ORDER = "7,0,1,2,3,57,52,59,51,5,6,8,11,10,53,12,50,33,13,36,14,46,47,48,34,58,18,16,22,17,76,19,23,21,20,9,28,44,15,37,24,25,26,38,129,62,72,39,27,73,49,63,45,85,87,88,128,41,89,35,86,90,74,96,118,117,98,99,97,64,75,65,4,93,91,30,92,94,29,43,100,111,108,116,95,66,67,68,69,70,60,71,61,103,119,104,101,105,126,102,40,127,106,120,109,42,107,110,112,113,114,121,77,122,123,54,84,146,133,130,147,31,148,151,141,124,149,125,134,131,115,150,152,153,154,138,132,135,160,155,161,162,156,214,142,157,158,143,163,173,164,139,137,140,174,32,136,144,165,166,78,167,170,168,171,169,175,215,222,172,178,81,179,181,218,80,180,219,216,176,145,182,177,185,232,192,183,184,243,225,220,186,217,193,187,194,205,195,188,223,189,226,196,190,197,198,199,202,200,221,206,224,227,228,203,201,207,210,159,253,79,204,55,211,256,229,212,230,83,213,191,233,254,257,208,234,284,252,260,240,241,308,261,242,82,235,56,247,263,309,209,244,270,245,248,246,231,249,264,255,262,258,259,236,265,266,237,267,250,251,268,271,269,273,238,293,278,272,281,239,274,275,288,276,289,294,282,283,285,339,338,279,286,295,287,290,296,280,297,277,299,298,291,292,306,307,300,303,301,304,302,318,310,326,305,313,314,311,321,322,319,327,328,329,315,312,323,320,330,333,331,334,332,348,317,316,324,356,335,357,343,340,359,358,361,325,360,363,364,351,362,370,336,344,341,365,371,372,373,374,345,342,347,346,383,366,349,367,350,368,352,353,384,354,369,375,376,377,380,378,379,385,381,388,425,435,337,389,382,391,390,428,426,355,424,392,395,386,402,393,394,432,396,427,403,436,397,404,398,399,429,453,405,415,462,406,387,400,416,433,430,442,431,437,434,438,407,408,409,417,410,411,420,421,412,422,413,466,423,439,414,440,418,443,467,518,470,471,463,419,464,444,450,451,452,480,494,473,519,454,445,457,455,458,456,441,472,468,465,446,469,459,460,461,474,401,447,475,476,448,477,449,478,483,481,484,482,498,479,503,485,488,489,491,492,549,504,486,493,505,499,495,548,496,497,500,506,490,507,508,501,502,509,487,516,510,517,511,513,512,514,520,536,531,523,515,524,525,528,521,532,522,529,538,537,533,530,539,540,543,526,534,527,535,541,544,542,545,558,553,566,561,550,567,554,569,568,562,570,571,573,572,580,546,551,563,574,575,581,576,582,577,583,584,559,593,634,552,578,555,556,585,586,560,594,547,587,579,588,590,589,564,557,635,638,598,645,565,591,599,592,601,600,603,602,605,604,636,639,612,642,637,607,595,596,597,606,608,613,614,609,615,616,625,610,640,646,647,626,641,643,617,644,618,619,622,620,627,623,621,648,679,708,652,663,630,631,687,680,683,690,649,624,611,628,650,688,653,651,684,689,681,691,655,632,656,685,654,682,686,692,629,657,667,633,673,658,660,693,661,697,694,662,695,698,668,664,665,674,659,666,675,700,699,705,706,676,707,709,677,678,669,710,712,670,671,711,713,714,718,696,701,702,719,703,704,720,721,715,722,716,723,672,717"
+
+
+def relay_of(src, dst, topo):
+    if topo.may_write(src, dst):
+        return None
+    can = [c for c in topo.cores_of(src) if topo.may_write(c, dst)]
+    near = [c for c in can if topo.die(c) == topo.die(src)]
+    return (near or can)[0]
+
+
+def mask_of(engines):
+    m = 0
+    for e in engines:
+        m |= 1 << e
+    return m
+
+
+def relay_program(g, core, T, topo, dst):
+    eng = topo.engines(core, dst)
+    rid, pid = topo.addr(dst, core)
+    n = 0
+    for t in range(NV - 1):
+        for h in range(NH):
+            c0 = 256 * t + CW * h
+            g.wait_ge(T.sem["hop%d%d" % (t, h)], len(eng))
+            g.remote_dma(T.w16[:, 256 + c0:256 + c0 + CW], T.wo[:, c0:c0 + CW], T.sem["arr%d%d" % (t, h)],
+                         T.sem.sent, pid, rid, mask_of(eng))
+            n += len(eng)
+    g.wait_ge(T.sem.sent, n)
+
+
+def build(g, core, T, topo):
+    ops = []
+    cur = [None]
+    N = len(T.cores)
+    rank = T.rank_of(core)
+    nxt = T.cores[(rank + 1) % N]
+    home = T.cores[(rank - (NV - 1)) % N]
+    rel = relay_of(core, nxt, topo)
+    eng_far = topo.engines(core, home)
+
+    def op(e, cost, r, w, fn, bank=None, sem=None):
+        ops.append((e, cost, list(r), list(w), bank, fn, sem, cur[0]))
+
+    def V(n, r, w, fn, bank=None):
+        op("v", max(64.0, n), r, w, fn, bank)
+
+    def S(n, r, w, fn, bank=None):
+        op("s", max(64.0, n), r, w, fn, bank)
+
+    def VG(n, r, w, fn, k="g"):
+        op("v", 60 + PAR[k] * n, r, w, fn)
+
+    def SG(n, r, w, fn):
+        op("s", 78 + PAR["g"] * n, r, w, fn)
+
+    def P(bank, r, mm):
+        cost = 0.0
+        for m in mm:
+            cost += max(64, m[5]) * PAR["pe"] * (4 if len(m) > 6 else 1)
+        op("p", cost, r, [], lambda e: [e.matmul(m[0], m[1], m[2], m[3], m[4]) for m in mm], bank)
+
+    def G(n, r, w, fn):
+        op("g", 150 + 2 * n, r, w, fn)
+
+    nd = [0]
+
+    def D(nbytes, r, w, out, in_):
+        op("y", 2000 + nbytes / 180.0, r, w, lambda e: e.dma_start(out, in_), None, "d%d" % nd[0])
+        nd[0] += 1
+
+    mat_at = {}
+
+    def mat(name):
+        if name not in mat_at:
+            mat_at[name] = len(mat_at)
+        return T.mats[:, 128 * mat_at[name]:128 * mat_at[name] + 128]
+
+    def B(name, h):
+        return T["%s%d" % (name, h)]
+
+    xw = [T.xa, T.xb]
+    xn = ["xa", "xb"]
+
+    def xres(b):
+        return [xn[b] + str(k) for k in range(NH)] + [xn[b] + "e"]
+
+    WN = ["wn%s%d" % (z, k) for z in "ab" for k in range(NH)]
+
+    D(131072, [], ["wi"], T.wi[:], T.wd[:])
+    D(524288, [], xres(0)[:NH], T.xa[:, 0:2048], T.xt[:])
+    D(8192, [], ["xae"], T.xa[:, 2048:2080], T.xt[:, 0:32])
+    D(512, [], ["wti"], T.wti[:, 0:1], T.wt[:])
+    D(262144, ["xa0"], ["pi"], T.pi[:], T.pd[:])
+
+    G(128, [], ["ia"], lambda e: e.iota(T.ia[:], [[-1, 128]], 128, 1))
+    G(128, [], ["ib"], lambda e: e.iota(T.ib[:], [[-16, 8], [0, 16]], 0, 1))
+    V(128, [], ["one32"], lambda e: e.memset(T.one32[:], 1.0))
+    G(128, ["one32"], ["i32m"], lambda e: e.affine_select(T.i32m[:], T.one32[:], [[-1, 128]], A.is_equal, 0.0, 0, 1))
+    G(160, [], ["ic"], lambda e: e.iota(T.ic[:], [[1, 160]], 0, -1))
+    G(CW, [], ["idd"], lambda e: e.iota(T.idd[:, 0:CW], [[256, NC], [1, 16]], -4096, 0))
+    G(16, [], ["ie"], lambda e: e.iota(T.ie[:], [[16, 16]], 0, 0))
+    V(128, ["ia"], ["ia"], lambda e: e.tensor_scalar(T.ia[:], T.ia[:], 15, None, A.bitwise_and))
+    V(128, ["ib"], ["ib"], lambda e: e.tensor_scalar(T.ib[:], T.ib[:], -16, None, A.bitwise_and))
+    V(256, ["ia", "ib"], ["rr"], lambda e: e.tensor_tensor(T.rr[:], T.ia[:], T.ib[:], A.add))
+    V(128, ["rr"], ["up"], lambda e: e.tensor_scalar(mat("up"), T.rr[:], 1.0, None, A.is_equal))
+    V(128, ["rr"], ["dn"], lambda e: e.tensor_scalar(mat("dn"), T.rr[:], 15.0, None, A.is_equal))
+    V(128, ["rr"], ["dn2"], lambda e: e.tensor_scalar(mat("dn2"), T.rr[:], 14.0, None, A.is_equal))
+    V(128, ["ib"], ["o"], lambda e: e.tensor_scalar(mat("o"), T.ib[:], 0.0, None, A.is_equal))
+
+    def scaled(name, src, rs, k):
+        S(128, [rs], [name], lambda e: e.activation(mat(name), src, F.Copy, scale=float(k)))
+
+    scaled("ni", T.i32m[:], "i32m", -1)
+    scaled("id", T.i32m[:], "i32m", 1)
+    scaled("n8k", T.i32m[:], "i32m", -8192)
+    scaled("ihi", T.i32m[:], "i32m", 3232)
+    scaled("ilo", T.i32m[:], "i32m", 2080)
+    scaled("uphi", mat("up"), "up", 3232)
+    scaled("uplo", mat("up"), "up", 2080)
+    scaled("ohi", mat("o"), "o", 1616)
+    scaled("olo", mat("o"), "o", 1040)
+    scaled("oh", mat("o"), "o", 0.5)
+    V(256, ["id", "up"], ["tm"], lambda e: e.tensor_tensor(mat("tm"), mat("id"), mat("up"), A.subtract))
+    V(256, ["dn2", "dn"], ["tq"], lambda e: e.tensor_tensor(mat("tq"), mat("dn2"), mat("dn"), A.subtract))
+    V(256, ["dn", "id"], ["tp"], lambda e: e.tensor_tensor(mat("tp"), mat("dn"), mat("id"), A.subtract))
+    S(128, ["tp"], ["sw32"], lambda e: e.activation(T.sw32[:], mat("tp"), F.Copy, scale=-0.5))
+    V(1, ["ia"], ["c0"], lambda e: e.tensor_copy(T.cols[:, 0:1], T.ia[:, 0:1]))
+    V(1, ["ia"], ["c1"], lambda e: e.tensor_scalar(T.cols[:, 1:2], T.ia[:, 0:1], 16.0, None, A.mult))
+    V(1, ["wti"], ["c3"], lambda e: e.tensor_copy(T.cols[:, 3:4], T.wti[:, 0:1]))
+    V(16, ["ia"], ["c16"], lambda e: e.tensor_scalar(T.cols[:, 16:32], T.ia[:, 0:16], 0.0, 2.0, A.is_equal, A.mult))
+    V(160, ["ic", "c0"], ["eb"], lambda e: e.tensor_scalar(T.eb[:], T.ic[:], T.cols[:, 0:1], 16.0, A.add, A.is_equal))
+    S(160, ["eb"], ["en"], lambda e: e.activation(T.en[:], T.eb[:], F.Copy, scale=-2048.0))
+    S(160, ["eb"], ["ep"], lambda e: e.activation(T.ep[:], T.eb[:], F.Copy, scale=4096.0))
+    S(160, ["eb", "c3"], ["ew"], lambda e: e.activation(T.ew[:], T.eb[:], F.Identity, scale=T.cols[:, 3:4]))
+    V(290, ["eb"], ["dbig"], lambda e: e.tensor_tensor(T.dbig[:, 1:145], T.eb[:, 2:146], T.eb[:, 0:144], A.subtract))
+
+    def esl(buf, m):
+        return buf[:, 16 - m:144 - m]
+
+    V(256, ["eb"], ["d0"], lambda e: e.tensor_tensor(mat("d0"), esl(T.eb, 15), esl(T.eb, 1), A.subtract))
+    V(256, ["eb"], ["d15"], lambda e: e.tensor_tensor(mat("d15"), esl(T.eb, 14), esl(T.eb, 0), A.subtract))
+
+    def dk(k):
+        return mat("d0") if k == 0 else mat("d15") if k == 15 else esl(T.dbig, k)
+
+    V(CW, ["idd", "c1"], ["ck"], lambda e: e.tensor_scalar(T.ck[:], T.idd[:, 0:CW], T.cols[:, 1:2], None, A.add))
+    V(CW, ["ck"], ["cke"], lambda e: e.tensor_scalar(T.cke[:], T.ck[:], -4096.0 * 4080, None, A.add))
+    for a, v in enumerate((15, 1, 0, 0)):
+        S(CW, ["one32", "c16"], ["coh%d" % a], lambda e, a=a, v=v: e.activation(
+            T.coh[:, CW * a:CW * a + CW], T.one32[:, 0:CW], F.Identity, scale=T.cols[:, 16 + v:17 + v]))
+    V(64, [], ["cac0"], lambda e: e.memset(T.cac[:, 0:CW], 2080.0))
+    V(64, [], ["cac1"], lambda e: e.memset(T.cac[:, CW:2 * CW], 3232.0))
+    V(CW, [], ["msk"], lambda e: e.memset(T.msk[:], 1.0))
+    V(NC, [], ["msk"], lambda e: e.memset(T.msk[:, 0:CW:16], 0.0))
+    V(512, [], WN, lambda e: e.memset(T.wn[:], 0.0))
+    V(64, [], ["oneb"], lambda e: e.memset(T.oneb[:], 1.0))
+    V(1, [], ["gdc"], lambda e: e.memset(T.gd[:, 16:17], 31.0 / 256))
+    V(1, [], ["acol"], lambda e: e.memset(T.acol[:, 0:1], 0.0))
+    if EXP:
+        G(CW, [], ["ig"], lambda e: e.iota(T.ig[:, 0:CW], [[16, CW]], 0, 0))
+        V(CW, ["ig", "c0"], ["cz"], lambda e: e.tensor_scalar(T.cz[:], T.ig[:, 0:CW], T.cols[:, 0:1], None, A.add))
+        V(CW, ["ia"], ["dia"], lambda e: e.tensor_scalar(T.dia[:], T.ia[:, 0:CW], 0.0, None, A.is_equal))
+        V(16, ["ie"], ["lc"], lambda e: e.tensor_scalar(T.lc[:], T.ie[:], 1.0 / 16, None, A.mult))
+        scaled("o8k", mat("o"), "o", 8192)
+    else:
+        V(CW, ["one32", "c0"], ["cz"], lambda e: e.tensor_scalar(T.cz[:], T.one32[:, 0:CW], T.cols[:, 0:1], None, A.mult))
+        V(64, [], ["c8k"], lambda e: e.memset(T.c8k[:], 8192.0))
+        for m in range(16):
+            G(128, ["c8k"], ["rm%d" % m], lambda e, m=m: e.affine_select(
+                T.rm[:, 128 * m:128 * m + 128], T.c8k[:], [[-16, 8], [0, 16]], A.is_equal, 0.0, -m, 1))
+    V(16, ["ie", "c0"], ["ti"], lambda e: e.tensor_scalar(T.ti[:], T.ie[:], T.cols[:, 0:1], None, A.add))
+    if not EXP:
+        V(16, ["ti"], ["b16"], lambda e: e.tensor_scalar(T.b16[:], T.ti[:], 16.0, None, A.mult))
+    V(16, ["ti"], ["ct"], lambda e: e.tensor_scalar(T.ct[:], T.ti[:], 32.0, -2048.0 * 8164 - 1024, A.mult, A.add))
+    for h in range(NH):
+        V(16, ["ti"], ["cb%d" % h], lambda e, h=h: e.tensor_scalar(
+            T.cb[:, NC * h:NC * h + NC], T.ti[:, 0:NC], 8.0, None, A.mult))
+    V(16, ["ti"], ["cbd"], lambda e: e.tensor_scalar(T.cb[:, 16:32], T.ti[:], -512.0, None, A.add))
+    V(16, ["ti"], ["t256"], lambda e: e.tensor_scalar(T.t256[:], T.ti[:], 1.0 / 256, 1.0, A.mult, A.add))
+    V(16, ["ti"], ["lsb"], lambda e: e.tensor_scalar(T.lsb[:], T.ti[:], 512.0, None, A.add))
+    V(512, ["pi"], ["sw"], lambda e: e.tensor_scalar(T.sw[:, 0:512], T.pi[:], -2048.0, None, A.add))
+    for h in range(NH):
+        V(CW, ["wi"], ["w0%d" % h], lambda e, h=h: e.tensor_scalar(
+            T.w16[:, CW * h:CW * h + CW], T.wi[:, CW * h:CW * h + CW], -2048.0, None, A.add))
+
+    def finish_lists(h, st):
+        p1, b1, xi, p32 = B("ps%d" % h, 1), "p%d1" % h, B("xi", h), B("p32", h)
+        for z, c in (("a", 0), ("b", CW)):
+            pz, c2 = ("a", 0) if st == 0 else (z, c)
+            k = "xi%s%d" % (z, h)
+            V(CW, ["p32%s%d" % (pz, h)], [k], lambda e, c=c, c2=c2: e.tensor_tensor(
+                xi[:, c:c + CW], p1[:, c:c + CW], p32[:, c2:c2 + CW], A.add), b1)
+            V(CW, [k], [k], lambda e, c=c: e.tensor_scalar(
+                xi[:, c:c + CW], xi[:, c:c + CW], 5, 2047, A.arith_shift_right, A.bitwise_and))
+            V(CW, ["acol", k], ["off%s%d" % (z, h)], lambda e, c=c: e.tensor_scalar(
+                B("off", h)[:, c:c + CW], xi[:, c:c + CW], T.acol[:, 0:1], None, A.add))
+
+    def gathers(t, st, h):
+        x = xw[t % 2]
+        ph = "g%d%d" % (st, h)
+        cur[0] = (t, ph)
+        p2, p3 = B("ps%d" % h, 2), B("ps%d" % h, 3)
+        P("p%d2" % h, ["i32m", "ck", "cke"], [(p2[:, 0:CW], T.i32m[:], (T.cke if st else T.ck)[:], True, False, CW, 4)])
+        if st == 0:
+            P("p%d3" % h, ["n8k", "cz"], [(p3[:, 0:CW], mat("n8k"), T.cz[:], True, False, CW)])
+        for s in range(NS):
+            cur[0] = (t, ph, 0.01 * s - AHEAD)
+            a, b = 16 * SW * s, 16 * SW * (s + 1)
+            fb, db, ab, off = B("fb", h)[:, a:b], B("db", h)[:, a:b], B("ab", h), B("off", h)
+            o1, o2 = off[:, SW * s:SW * s + SW], off[:, CW + SW * s:CW + SW * s + SW]
+            k = "%d%d" % (h, s)
+            if (t, st, h, s) in FV:
+                VG(b - a, xres(t % 2) + ["offa%d" % h], ["fb" + k], lambda e, fb=fb, o1=o1: e.tensor_copy(fb, x[:].indirect(o1)))
+            else:
+                SG(b - a, xres(t % 2) + ["offa%d" % h], ["fb" + k],
+                   lambda e, fb=fb, o1=o1: e.activation(fb, x[:].indirect(o1), F.Copy))
+            VG(b - a, xres(t % 2) + ["offb%d" % h, "fb" + k], ["db" + k],
+               lambda e, fb=fb, db=db, o2=o2: e.tensor_tensor(db, x[:].indirect(o2), fb, A.subtract))
+            cur[0] = (t, ph, 0.01 * s - 0.005)
+            c0, c1 = SW // 16 * s, SW // 16 * (s + 1)
+            S(b - a, ["db" + k], ["ab" + k], lambda e, db=db, c0=c0, c1=c1: e.activation(ab[:, c0:c1], db, F.Abs))
+            if (s + 1) % NP:
+                continue
+            c0 = c1 - NP * SW // 16
+            AB = ["ab%d%d" % (h, z) for z in range(s + 1 - NP, s + 1)]
+            P("p%d2" % h, AB + ["en", "ep"],
+              [(p2[:, 16 * c0:16 * c1], esl(T.ep if st else T.en, m), ab[:, c0:c1, m, :], False,
+                s == NS - 1 and m == 15, NP * SW) for m in range(16)])
+            if st == 0:
+                P("p%d3" % h, AB + ["dbig", "d0", "d15"],
+                  [(p3[:, 16 * c0:16 * c1], dk(m), ab[:, c0:c1, :, m], False, False, NP * SW) for m in range(16)])
+
+    def pick(h, first):
+        p2, p3, rs, ix, kb = B("ps%d" % h, 2), B("ps%d" % h, 3), B("rs", h), B("ix", h), B("kb", h)
+        hs = str(h)
+        V(CW, ["msk"], ["rs" + hs], lambda e: e.tensor_tensor_scan(rs[:], T.msk[:], p2[:, 0:CW], 0.0, A.mult, A.min), "p%d2" % h)
+        V(NC, ["rs" + hs], ["ix" + hs], lambda e: e.tensor_scalar(ix[:, 0:NC], rs[:, 15:CW:16], 2047, None, A.bitwise_and))
+        V(NC, ["ix" + hs], ["lk" + hs], lambda e: e.tensor_copy(B("lk", h)[:, 0:NC], ix[:, 0:NC]))
+        if first:
+            P("p%d3" % h, ["n8k", "cz"], [(p3[:, 0:CW], mat("n8k"), T.cz[:], True, False, CW)])
+        if EXP:
+            VG(CW, ["ix" + hs, "lc", "dia"], ["kb" + hs], lambda e: e.tensor_tensor(
+                kb[:], ix[:, 0:NC].indirect(T.lc[:, 0:NC]), T.dia[:], A.mult))
+            P("p%d3" % h, ["kb" + hs, "o8k"], [(p3[:, 0:CW], mat("o8k"), kb[:], False, True, CW)])
+        else:
+            V(NC, ["ix" + hs, "b16"], ["kb" + hs], lambda e: e.tensor_tensor(kb[:, 0:NC], ix[:, 0:NC], T.b16[:, 0:NC], A.subtract))
+            P("p%d3" % h, ["kb" + hs] + ["rm%d" % m for m in range(16)],
+              [(p3[:, m:CW:16], T.rm[:, 128 * m:128 * m + 128], kb[:, 0:NC], False, m == 15, NC) for m in range(16)])
+
+    FB = lambda h: ["fb%d%d" % (h, s) for s in range(NS)]
+    DB = lambda h: ["db%d%d" % (h, s) for s in range(NS)]
+
+    def stage1(t, h):
+        w, wr = T.w16[:, 256 * t + CW * h:256 * t + CW * h + CW], "w%d%d" % (t, h)
+        p0, p1 = B("ps%d" % h, 0), B("ps%d" % h, 1)
+        b0, b1 = "p%d0" % h, "p%d1" % h
+        cur[0] = (t, "a%d" % h, -0.001)
+        P(b0, [wr, "up"], [(p0[:, 0:CW], mat("up"), w, True, True, CW)])
+        cur[0] = (t, "a%d" % h)
+        P(b1, [wr, "ihi", "ilo", "uphi", "uplo"],
+          [(p1[:, 0:CW], mat("ihi"), w, True, False, CW), (p1[:, 0:CW], mat("uplo"), w, False, True, CW),
+           (p1[:, CW:2 * CW], mat("ilo"), w, True, False, CW), (p1[:, CW:2 * CW], mat("uphi"), w, False, True, CW)])
+        V(CW, [wr], ["p32a%d" % h], lambda e: e.tensor_tensor(B("p32", h)[:, 0:CW], p0[:, 0:CW], w, A.mult), b0)
+        finish_lists(h, 0)
+        P(b0, [wr, "up", "ni"],
+          [(p0[:, CW:2 * CW], mat("up"), w, True, False, CW), (p0[:, CW:2 * CW], mat("ni"), w, False, True, CW)])
+        S(CW, [], ["dw%d" % h], lambda e: e.activation(B("dw", h)[:], p0[:, CW:2 * CW], F.Copy), b0)
+        gathers(t, 0, h)
+
+    def middle(t, h):
+        w, wr = T.w16[:, 256 * t + CW * h:256 * t + CW * h + CW], "w%d%d" % (t, h)
+        p0, p1, p2, p3 = [B("ps%d" % h, b) for b in range(4)]
+        b0, b1, b2, b3 = ["p%d%d" % (h, b) for b in range(4)]
+        gg, tt, p32, b32 = B("gg", h), B("tt", h), B("p32", h), B("b32", h)
+        hs = str(h)
+        pick(h, False)
+        SG(CW, FB(h) + ["lk" + hs], ["fk" + hs], lambda e: e.activation(
+            B("fk", h)[:], B("fb", h)[:].indirect(B("lk", h)[:, 0:NC]), F.Copy))
+        P(b2, ["fk" + hs, "ew"], [(p2[:, CW:CW + NC], esl(T.ew, m), B("fk", h)[:, m:CW:16], m == 0, m == 15, NC)
+                                  for m in range(16)])
+        S(CW, [], ["ga" + hs], lambda e: e.activation(gg[:, 0:CW], p3[:, 0:CW], F.Sign, bias=-0.5), b3)
+        S(CW, [], ["gb" + hs], lambda e: e.activation(gg[:, CW:2 * CW], p3[:, 0:CW], F.Sign, bias=-4096.0), b3)
+        ui = T.ui[:, NC * h:NC * h + NC]
+        V(NC, [], ["ui" + hs], lambda e: e.tensor_copy(ui, p2[:, CW:CW + NC]), b2)
+        V(NC, ["ui" + hs], ["u9" + hs], lambda e: e.tensor_scalar(B("u9", h)[:, 0:NC], ui, 511, None, A.bitwise_and))
+        V(NC, ["u9" + hs], ["lb" + hs], lambda e: e.tensor_copy(B("lb", h)[:, 0:NC], B("u9", h)[:, 0:NC]))
+        SG(CW, ["sw", "lb" + hs], ["b32" + hs], lambda e: e.activation(
+            b32[:], T.sw[:, 0:512].indirect(B("lb", h)[:, 0:NC]), F.Copy))
+        V(NC, ["rs" + hs, "ct"], ["th" + hs], lambda e: e.tensor_tensor(
+            B("th", h)[:, 0:NC], T.ct[:, 0:NC], B("rs", h)[:, 15:CW:16], A.subtract))
+        P(b0, ["ga" + hs, "id", "tm", "tq", "coh0", "coh1"],
+          [(p0[:, 0:2 * CW], mat("id"), T.coh[:, 0:2 * CW], True, False, 2 * CW),
+           (p0[:, 0:CW], mat("tm"), gg[:, 0:CW], False, False, CW),
+           (p0[:, CW:2 * CW], mat("tq"), gg[:, 0:CW], False, True, CW)])
+        V(CW, [wr], ["ta" + hs], lambda e: e.tensor_tensor(tt[:, 0:CW], p0[:, 0:CW], w, A.mult), b0)
+        V(CW, [wr], ["tb" + hs], lambda e: e.tensor_tensor(tt[:, CW:2 * CW], p0[:, CW:2 * CW], w, A.mult), b0)
+        P(b1, ["ta" + hs, "tb" + hs, "id", "cac0", "cac1", "oh"],
+          [(p1[:, 2 * CW:4 * CW], mat("id"), T.cac[:], True, False, 2 * CW),
+           (p1[:, 2 * CW:4 * CW], mat("oh"), tt[:], False, True, 2 * CW)])
+        P(b1, ["ta" + hs, "tb" + hs, "ohi", "olo"],
+          [(p1[:, 0:CW], mat("ohi"), tt[:, 0:CW], True, True, CW),
+           (p1[:, CW:2 * CW], mat("olo"), tt[:, CW:2 * CW], True, True, CW)])
+        V(CW, ["b32" + hs], ["p32a" + hs], lambda e: e.tensor_tensor(p32[:, 0:CW], p1[:, 2 * CW:3 * CW], b32[:], A.mult), b1)
+        V(CW, ["b32" + hs], ["p32b" + hs], lambda e: e.tensor_tensor(p32[:, CW:2 * CW], p1[:, 3 * CW:4 * CW], b32[:], A.mult), b1)
+        finish_lists(h, 1)
+        P(b0, ["ga" + hs, "gb" + hs, "id", "tp", "coh2", "coh3"],
+          [(p0[:, 2 * CW:4 * CW], mat("id"), T.coh[:, 2 * CW:4 * CW], True, False, 2 * CW),
+           (p0[:, 2 * CW:4 * CW], mat("tp"), gg[:], False, True, 2 * CW)])
+        S(CW, [], ["ohp" + hs], lambda e: e.activation(B("ohp", h)[:], p0[:, 2 * CW:3 * CW], F.Copy, scale=0.5), b0)
+        V(CW, ["dw" + hs], ["s32" + hs], lambda e: e.tensor_tensor(
+            B("s32", h)[:], p0[:, 3 * CW:4 * CW], B("dw", h)[:], A.mult), b0)
+        P(b3, ["s32" + hs, wr, "id", "sw32"],
+          [(p3[:, 3 * CW:4 * CW], mat("id"), w, True, False, CW),
+           (p3[:, 3 * CW:4 * CW], T.sw32[:], B("s32", h)[:], False, True, CW, 4)])
+        S(CW, [], ["wnb" + hs], lambda e: e.activation(
+            T.wn[:, 256 + CW * h:256 + CW * h + CW], p3[:, 3 * CW:4 * CW], F.Copy), b3)
+
+    def write_lists():
+        UI = ["ui%d" % h for h in range(NH)]
+        V(16, UI, ["sma"], lambda e: e.tensor_scalar(T.sm[:, 0:16], T.ui[:], 7, None, A.bitwise_and))
+        V(16, UI, ["smb"], lambda e: e.tensor_scalar(T.sm[:, 16:32], T.ui[:], 1, None, A.bitwise_and))
+        V(32, ["sma", "smb", "cbd"] + ["cb%d" % h for h in range(NH)], ["sm2"],
+          lambda e: e.tensor_tensor(T.sm2[:], T.sm[:], T.cb[:], A.add))
+        V(16, ["sm2"], ["lx"], lambda e: e.tensor_copy(T.lx[:], T.sm2[:, 0:16]))
+
+    def write_stock(t, hh):
+        a, b = NC * hh[0], NC * (hh[-1] + 1)
+        k = str(hh[0])
+        V(16, ["gd%d" % h for h in hh] + ["sm2"], ["g6" + k], lambda e: e.tensor_tensor(
+            T.g6[:, a:b], T.gd[:, a:b], T.sm2[:, 16 + a:16 + b], A.mult))
+        V(16, ["g6" + k, "lsb"], ["g6" + k], lambda e: e.tensor_tensor(T.g6[:, a:b], T.g6[:, a:b], T.lsb[:, a:b], A.add))
+        V(16, ["g6" + k], ["ls" + k], lambda e: e.tensor_copy(T.ls[:, a:b], T.g6[:, a:b]))
+        VG(16 * (b - a), ["wna%d" % h for h in hh] + ["ls" + k], ["sw"],
+           lambda e: e.tensor_copy(T.sw[:].indirect(T.ls[:, a:b]), T.wn[:, 16 * a:16 * b]), "s")
+        if t == NV - 1:
+            S(32 * (b - a), ["sw"], ["op" + k], lambda e: e.activation(
+                T.op[:, 32 * a:32 * b], T.sw[:, 32 * a:32 * b], F.Identity, bias=2048.0))
+            D(16384 * (b - a), ["op" + k], [], T.yp[:, 32 * a:32 * b], T.op[:, 32 * a:32 * b])
+
+    def ending(t, h):
+        w, wr = T.w16[:, 256 * t + CW * h:256 * t + CW * h + CW], "w%d%d" % (t, h)
+        p0, p1, p2, p3 = [B("ps%d" % h, b) for b in range(4)]
+        b0, b1, b2, b3 = ["p%d%d" % (h, b) for b in range(4)]
+        hs = str(h)
+        gg, lk, g7, lg, wn = B("gg", h), B("lk", h), B("g7", h), B("lg", h), T.wn
+        gd = T.gd[:, NC * h:NC * h + NC]
+        y, yr = xw[(t + 1) % 2], xn[(t + 1) % 2]
+        pick(h, True)
+        V(NC, ["rs" + hs, "th" + hs], ["gd" + hs], lambda e: e.tensor_tensor(
+            gd, B("rs", h)[:, 15:CW:16], B("th", h)[:, 0:NC], A.is_lt))
+        if h == NH - 1 and t < NV - 1:
+            ac = T.acol
+            P(b2, ["oneb", "gdc"] + ["gd%d" % k for k in range(NH)],
+              [(p2[:, CW:CW + 17], T.oneb[:], T.gd[:, 0:17], True, True, 17)])
+            V(17, [], ["an"], lambda e: e.tensor_reduce(ac[:, 4:5], p2[:, CW:CW + 17], X.X, A.add, negate=True), b2)
+            V(1, ["an"], ["aq"], lambda e: e.tensor_scalar(ac[:, 8:9], ac[:, 4:5], M5, -M5, A.add, A.add))
+            V(1, ["an", "aq"], ["acol"], lambda e: e.tensor_scalar(
+                ac[:, 0:1], ac[:, 4:5], ac[:, 8:9], 15.5, A.subtract, A.add))
+        SG(CW, DB(h) + ["lk" + hs], ["hf" + hs], lambda e: e.activation(
+            B("hf", h)[:], B("db", h)[:].indirect(lk[:, 0:NC]), F.Identity, bias=-0.25, scale=0.5))
+        VG(CW, FB(h) + ["lk" + hs, "hf" + hs], ["av" + hs], lambda e: e.tensor_tensor(
+            B("av", h)[:], B("fb", h)[:].indirect(lk[:, 0:NC]), B("hf", h)[:], A.add))
+        VG(CW, ["av" + hs, "lx"], [yr + hs], lambda e: e.tensor_copy(
+            y[:, 8 * CW * h:8 * CW * (h + 1)].indirect(T.lx[:, NC * h:NC * h + NC]), B("av", h)[:]), "s")
+        if t == NV - 1:
+            D(2048 * CW, [yr + hs], [], T.yx[:, 8 * CW * h:8 * CW * (h + 1)], y[:, 8 * CW * h:8 * CW * (h + 1)])
+        elif h == 0:
+            S(32, [yr + hs], [yr + "e"], lambda e: e.activation(y[:, 2048:2080], y[:, 0:32], F.Copy))
+        S(CW, [], ["ga" + hs], lambda e: e.activation(gg[:, 0:CW], p3[:, 0:CW], F.Sign, bias=-4096.0), b3)
+        P(b0, ["ga" + hs, "id", "tp", "coh2"],
+          [(p0[:, 0:CW], mat("id"), T.coh[:, 2 * CW:3 * CW], True, False, CW),
+           (p0[:, 0:CW], mat("tp"), gg[:, 0:CW], False, True, CW)])
+        V(CW, ["b32" + hs], ["bj" + hs], lambda e: e.tensor_tensor(B("bj", h)[:], p0[:, 0:CW], B("b32", h)[:], A.mult), b0)
+        P(b1, [wr, "ni", "id"],
+          [(p1[:, CW:2 * CW], mat("id"), w, True, True, CW), (p1[:, 0:CW], mat("ni"), w, True, False, CW)])
+        P(b1, ["bj" + hs, "oh"], [(p1[:, 0:CW], mat("oh"), B("bj", h)[:], False, True, CW)])
+        V(CW, ["ohp" + hs], ["tm" + hs], lambda e: e.tensor_tensor(B("tm", h)[:], p1[:, 0:CW], B("ohp", h)[:], A.mult), b1)
+        V(CW, ["tm" + hs], ["wna" + hs], lambda e: e.tensor_tensor(
+            wn[:, CW * h:CW * h + CW], p1[:, CW:2 * CW], B("tm", h)[:], A.add), b1)
+        V(NC, ["gd" + hs, "t256"], ["g7" + hs], lambda e: e.tensor_tensor(
+            g7[:, 0:NC], T.t256[:, NC * h:NC * h + NC], gd, A.subtract))
+        V(NC, ["g7" + hs], ["lg" + hs], lambda e: e.tensor_scalar(lg[:, 0:NC], g7[:, 0:NC], 256.0, None, A.mult))
+        arr = "arr%d%d" % (t, h)
+        if t < NV - 1:
+            c0 = 256 * t + CW * h
+            wo = T.wo[:, c0:c0 + CW]
+            VG(CW, WN + ["lg" + hs], ["wo%d%d" % (t, h)], lambda e: e.tensor_copy(wo, wn[:].indirect(lg[:, 0:NC])))
+            if rel is None:
+                to, land, rs, eng = nxt, T.w16[:, 256 + c0:256 + c0 + CW], arr, topo.engines(core, nxt)
+            else:
+                to, land, rs, eng = rel, wo, "hop%d%d" % (t, h), eng_far
+            rid, pid = topo.addr(to, core)
+            op("r", 300, ["wo%d%d" % (t, h)], ["sent%d%d" % (t, h)], lambda e: e.remote_dma(
+                land, wo, T.sem[rs], T.sem.sent, pid, rid, mask_of(eng)), None, len(eng))
+            op("n", PAR["far"], ["sent%d%d" % (t, h)], ["w%d%d" % (t + 1, h)], None, None, (arr, len(eng_far)))
+        else:
+            VG(CW, WN + ["lg" + hs], ["wf" + hs], lambda e: e.tensor_scalar(
+                B("wf", h)[:], wn[:].indirect(lg[:, 0:NC]), 2048.0, None, A.add))
+            rid, pid = topo.addr(home, core)
+            op("r", 300, ["wf" + hs], ["sent%d%d" % (t, h)], lambda e: e.remote_dma(
+                B("lf", h)[:], B("wf", h)[:], T.sem[arr], T.sem.sent, pid, rid, mask_of(eng_far)), None, len(eng_far))
+            op("n", 0.6 * PAR["far"], ["sent%d%d" % (t, h)], ["lf" + hs], None, None, (arr, len(eng_far)))
+            D(512 * CW, ["lf" + hs], [], T.yw[:, CW * h:CW * h + CW], B("lf", h)[:])
+            cur[0] = (t, "z0")
+            write_stock(t, [h])
+
+    for t in range(NV):
+        for h in range(NH):
+            stage1(t, h)
+            if h == 0:
+                D(524288, ["offa0"] + xres(t % 2)[:NH], xres((t + 1) % 2)[:NH], xw[(t + 1) % 2][:, 0:2048],
+                  T.xt[:] if t == 0 else xw[t % 2][:, 0:2048])
+        for h in range(NH):
+            cur[0] = (t, "m%d" % h)
+            middle(t, h)
+        write_lists()
+        for h in range(NH):
+            gathers(t, 1, h)
+            cur[0] = (t, "e%d" % h)
+            ending(t, h)
+        if t < NV - 1:
+            cur[0] = (t, "z0")
+            write_stock(t, list(range(NH)))
+    return ops
+
+
+QUEUE = {"v": "v", "s": "s", "p": "p", "g": "g", "r": "g", "y": "y", "n": "n"}
+
+
+def plan(ops):
+    n = len(ops)
+    deps = [set() for _ in range(n)]
+    soft = [set() for _ in range(n)]
+    wr, rd, bk = {}, {}, {}
+    for i, (e, c, r, w, bank, fn, sem, key) in enumerate(ops):
+        for k in r:
+            if k in wr:
+                deps[i].add(wr[k])
+        for k in w:
+            if k in wr:
+                deps[i].add(wr[k])
+            deps[i].update(rd.get(k, []))
+        for k in r:
+            rd.setdefault(k, []).append(i)
+        for k in w:
+            wr[k] = i
+            rd[k] = []
+        if bank:
+            run, before = bk.get(bank, ([], []))
+            if run and ops[run[0]][0] == e:
+                soft[i].add(run[-1])
+                deps[i].update(before)
+                run.append(i)
+            else:
+                deps[i].update(run)
+                bk[bank] = ([i], run)
+        deps[i].discard(i)
+    users = [[] for _ in range(n)]
+    for i in range(n):
+        for j in deps[i] | soft[i]:
+            users[j].append(i)
+    lat = PAR["lat"]
+    chain = [0.0] * n
+    for i in range(n - 1, -1, -1):
+        chain[i] = ops[i][1] + lat + max([chain[j] for j in users[i]] + [0.0])
+    rank = [1e9 if o[7] is None else 10 * o[7][0] + KEYS[o[7][1]] + sum(o[7][2:]) for o in ops]
+    for i in range(n - 1, -1, -1):
+        rank[i] = min([rank[i]] + [rank[j] for j in users[i]])
+    prio = [(-rank[i], chain[i] * (1.0 + JIT[1] * (((i + 1) * JIT[0] * 0.6180339887) % 1.0))) for i in range(n)]
+    hold = lambda i: 60.0 if ops[i][0] == "y" else 0.0 if ops[i][0] == "n" else ops[i][1]
+    free = {q: 0.0 for q in QUEUE.values()}
+    left = [len(deps[i] | soft[i]) for i in range(n)]
+    ready_at = [0.0] * n
+    ready = [i for i in range(n) if left[i] == 0]
+    order, end, start = [], [0.0] * n, [0.0] * n
+    while ready:
+        t0, q0 = min((max(ready_at[i], free[QUEUE[ops[i][0]]]), QUEUE[ops[i][0]]) for i in ready)
+        cand = [i for i in ready if QUEUE[ops[i][0]] == q0]
+        i = max([i for i in cand if ready_at[i] <= t0], key=lambda j: (prio[j], -j))
+        soon = [j for j in cand
+                if ready_at[j] > t0 and prio[j] > prio[i] and ready_at[j] - t0 < min(SOON[0], SOON[1] * hold(i))]
+        if soon:
+            i = max(soon, key=lambda j: (prio[j], -j))
+        ready.remove(i)
+        start[i] = max(t0, ready_at[i])
+        end[i] = start[i] + ops[i][1]
+        free[q0] = start[i] + hold(i)
+        order.append(i)
+        for j in users[i]:
+            ready_at[j] = max(ready_at[j], end[i] + lat if i in deps[j] else start[i])
+            left[j] -= 1
+            if left[j] == 0:
+                ready.append(j)
+    return order, deps, start, end, soft
+
+
+def rank_program(g, core, T, topo):
+    N = len(T.cores)
+    if T.rank_of(core) is None:
+        for r in range(N):
+            src, dst = T.cores[r], T.cores[(r + 1) % N]
+            if relay_of(src, dst, topo) == core:
+                relay_program(g, core, T, topo, dst)
+        return
+    ops = build(g, core, T, topo)
+    if "order" not in PLAN:
+        PLAN["order"] = plan(ops)
+    order, deps = PLAN["order"][0:2]
+    if ORDER:
+        order = [int(x) for x in ORDER.split(",")]
+        assert sorted(order) == list(range(len(ops)))
+        at = {i: k for k, i in enumerate(order)}
+        assert all(at[j] < at[i] for i in order for j in deps[i] | PLAN["order"][4][i])
+    eng = {"v": g.vector, "s": g.scalar, "p": g.tensor, "g": g, "r": g, "y": g.sync}
+    count = {"v": 0, "s": 0, "p": 0, "g": 0}
+    done = {}
+    seen = {q: {} for q in "vspgy"}
+    sent = 0
+    for i in order:
+        e, c, r, w, bank, fn, sem, key = ops[i]
+        if e == "n":
+            done[i] = sem
+            continue
+        need = {}
+        for j in deps[i]:
+            s, v = done[j]
+            need[s] = max(need.get(s, 0), v)
+        for s in sorted(need):
+            if seen[QUEUE[e]].get(s, 0) < need[s]:
+                eng[e].wait_ge(T.sem[s], need[s])
+                seen[QUEUE[e]][s] = need[s]
+        out = fn(eng[e])
+        if e == "r":
+            sent += sem
+            done[i] = ("sent", sent)
+        elif e == "y":
+            out.then_inc(T.sem[sem], 16)
+            done[i] = (sem, 16)
+        else:
+            for ins in (out if e == "p" else [out]):
+                ins.then_inc(T.sem["c" + e], 1)
+                count[e] += 1
+            done[i] = ("c" + e, count[e])
+    g.wait_ge(T.sem.sent, sent)
+    last = {}
+    for i in order:
+        s, v = done[i]
+        if s != "sent":
+            last[s] = max(last.get(s, 0), v)
+    for s in sorted(last):
+        if seen["y"].get(s, 0) < last[s]:
+            g.sync.wait_ge(T.sem[s], last[s])

@@ -1,64 +1,69 @@
+import math
 from concourse.mybir import AluOpType as A, ActivationFunctionType as F, AxisListType as X
 
 NV = 3
-NH = 2
-CW = 256 // NH
-NC = CW // 16
-NS = 4
-NP = 2
-SW = CW // NS
-EXP = False
+PARTS = [(0, 96), (96, 160), (160, 256)]
+NH = len(PARTS)
+PIECES = {(0, 0): "32A+ 32a+ 32a", (0, 1): "32a+ 32a", (0, 2): "32a+ 32a+ 32a",
+          (1, 0): "32a+ 32a+ 32a", (1, 1): "32a+ 32a", (1, 2): "32a+ 48a 16a"}
+BANKS = [(0, 1, 1, 1), (2, 3, 3, 3), (4, 5, 5, 5)]
+SPLIT = [(0, 0), (1, 0), (0, 2), (1, 2)]
+ON_VECTOR = "bz0 bz1 bz2"
+STOCK = [(0, 256)]
+COUNT = 7
+K = 8192.0
 M5 = 1.5 * 2.0 ** 28
 
 f32, bf, f16, i32, u16 = "float32", "bfloat16", "float16", "int32", "uint16"
+MATS = ["id", "up", "o", "ni", "ihi", "ilo", "uphi", "uplo", "um", "tm", "tp2", "tpk", "tq", "sk",
+        "ohi", "olo"]
+BANDS = {"en": 0, "ep": 160, "ew": 320, "dd": 480, "d0": 640, "d15": 768}
 SCRATCH = {
     "wi": ("sbuf", [128, 256], i32), "pi": ("sbuf", [128, 512], i32), "wti": ("sbuf", [128, 4], i32),
-    "xa": ("sbuf", [128, 2080], bf), "xb": ("sbuf", [128, 2080], bf),
-    "sw": ("sbuf", [128, 768], f32), "op": ("sbuf", [128, 512], f32), "wn": ("sbuf", [128, 512], f32),
-    "ia": ("sbuf", [128, 128], i32), "ib": ("sbuf", [128, 128], i32), "ic": ("sbuf", [128, 160], i32),
-    "idd": ("sbuf", [128, 128], i32), "ie": ("sbuf", [128, 16], i32), "ig": ("sbuf", [128, 128], i32),
-    "rr": ("sbuf", [128, 128], f32),
-    "one32": ("sbuf", [128, 128], f32), "oneb": ("sbuf", [128, 128], bf), "c8k": ("sbuf", [128, 128], bf),
-    "i32m": ("sbuf", [128, 128], f32), "sw32": ("sbuf", [128, 128], f32),
-    "mats": ("sbuf", [128, 24 * 128], bf), "rm": ("sbuf", [128, 16 if EXP else 16 * 128], bf),
-    "eb": ("sbuf", [128, 160], bf), "en": ("sbuf", [128, 160], bf), "ep": ("sbuf", [128, 160], bf),
-    "ew": ("sbuf", [128, 160], bf), "dbig": ("sbuf", [128, 160], bf),
-    "ck": ("sbuf", [128, CW], f32), "cke": ("sbuf", [128, CW], f32),
-    "cz": ("sbuf", [128, CW], f16), "coh": ("sbuf", [128, 4 * CW], bf), "cac": ("sbuf", [128, 2 * CW], bf),
-    "msk": ("sbuf", [128, CW], f32), "dia": ("sbuf", [128, CW], bf), "cols": ("sbuf", [128, 32], f32),
-    "ti": ("sbuf", [128, 16], f32), "b16": ("sbuf", [128, 16], f32), "ct": ("sbuf", [128, 16], f32),
-    "cb": ("sbuf", [128, 32], f32), "lsb": ("sbuf", [128, 16], f32), "t256": ("sbuf", [128, 16], f32),
-    "gd": ("sbuf", [128, 32], bf), "acol": ("sbuf", [128, 16], f32),
-    "ui": ("sbuf", [128, 16], i32), "sm": ("sbuf", [128, 32], i32), "sm2": ("sbuf", [128, 32], f32),
-    "lx": ("sbuf", [128, 16], u16), "g6": ("sbuf", [128, 16], f32), "ls": ("sbuf", [128, 16], u16),
-    "lc": ("sbuf", [128, 16], u16),
+    "x0": ("sbuf", [128, 2096], bf), "x1": ("sbuf", [128, 2096], bf),
+    "sw0": ("sbuf", [128, 1024], f32), "sw1": ("sbuf", [128, 1024], f32),
+    "op": ("sbuf", [128, 512], f32),
+    "mats": ("sbuf", [128, 128 * len(MATS)], bf), "imd": ("sbuf", [128, 128], f32),
+    "rm": ("sbuf", [128, 16 * 128], bf), "bands": ("sbuf", [128, 896], bf),
+    "one": ("sbuf", [128, 128], bf), "c8k": ("sbuf", [128, 128], bf), "cs": ("sbuf", [128, 256], bf),
+    "bz": ("sbuf", [128, 512], f32), "cm": ("sbuf", [128, 256], bf), "coh": ("sbuf", [128, 256], bf),
+    "ck": ("sbuf", [128, 256], f16), "msk": ("sbuf", [128, 128], bf),
+    "ia": ("sbuf", [128, 16], i32), "ic": ("sbuf", [128, 128], i32), "ie": ("sbuf", [128, 32], i32),
+    "cols": ("sbuf", [128, 32], f32), "tl": ("sbuf", [128, 16], f32), "b16": ("sbuf", [128, 16], f32),
+    "ct": ("sbuf", [128, 16], f32), "cb": ("sbuf", [128, 16], f32), "t2": ("sbuf", [128, 16], f32),
+    "sc": ("sbuf", [128, 2, 16], f32), "sx": ("sbuf", [128, 2, 16], f32), "hh": ("sbuf", [128, 2, 16], f32),
+    "ls": ("sbuf", [128, 2, 16], u16), "gd": ("sbuf", [128, 32], bf), "acol": ("sbuf", [128, 16], f32),
+    "ui": ("sbuf", [128, 16], i32), "sm": ("sbuf", [128, 32], i32), "sm2": ("sbuf", [128, 16], f32),
+    "lx": ("sbuf", [128, 16], u16), "ix": ("sbuf", [128, 16], i32), "lk": ("sbuf", [128, 16], u16),
+    "kb": ("sbuf", [128, 16], bf), "th": ("sbuf", [128, 16], f32), "u9": ("sbuf", [128, 16], i32),
+    "lb": ("sbuf", [128, 16], u16), "g7": ("sbuf", [128, 16], f32), "lg": ("sbuf", [128, 16], u16),
     "w16": ("sbuf", [128, NV * 256], f16),
     "wo": ("sbuf", [128, (NV - 1) * 256], f16),
+    "wf": ("sbuf", [128, 256], f32), "lf": ("sbuf", [128, 256], f32),
 }
-for _h in range(NH):
-    for _n, _w, _d in (("p32", 2 * CW, f32), ("dw", CW, f32), ("xi", 2 * CW, i32), ("off", 2 * CW, u16),
-                       ("fb", 16 * CW, bf), ("db", 16 * CW, bf), ("rs", CW, i32), ("ix", 16, i32),
-                       ("lk", 16, u16), ("kb", CW, f16), ("th", 16, f32), ("gg", 2 * CW, bf), ("fk", CW, bf),
-                       ("u9", 16, i32), ("lb", 16, u16), ("b32", CW, f32), ("tt", 2 * CW, f16), ("s32", CW, f32),
-                       ("ohp", CW, bf), ("g7", 16, f32), ("lg", 16, u16), ("bj", CW, f16), ("tm", CW, f32),
-                       ("hf", CW, f32), ("av", CW, i32), ("wf", CW, f32), ("lf", CW, f32)):
-        SCRATCH["%s%d" % (_n, _h)] = ("sbuf", [128, _w], _d)
-    SCRATCH["ab%d" % _h] = ("sbuf", [128, NC, 16, 16], bf)
-    for _b in range(4):
-        SCRATCH["ps%d%d" % (_h, _b)] = ("psum", [128, 512], f32)
+for _n, _d in (("rs", i32), ("ga", bf), ("gb", bf), ("fk", bf), ("r1", f32), ("wz", f32), ("bj", f16), ("hf", f32),
+               ("av", i32)):
+    SCRATCH[_n] = ("sbuf", [128, 256], _d)
+for _h, (_a, _b) in enumerate(PARTS):
+    _n = _b - _a
+    for _s, _w, _d in (("off", 2 * _n, u16), ("xi", 2 * _n, i32), ("xj", 4 * _n, i32), ("p32", _n, f32),
+                       ("tt", 2 * _n, f16),
+                       ("fb", 16 * _n, bf), ("db", 16 * _n, bf)):
+        SCRATCH["%s%d" % (_s, _h)] = ("sbuf", [128, _w], _d)
+    SCRATCH["ab%d" % _h] = ("sbuf", [128, _n // 16, 16, 16], bf)
+for _b in range(8):
+    SCRATCH["ps%d" % _b] = ("psum", [128, 512], f32)
 
-SEMAPHORES = (["cv", "cs", "cp", "cg", "sent"] + ["d%d" % k for k in range(16)]
+SEMAPHORES = (["cv", "cs", "cp", "cg", "sent"] + ["d%d" % k for k in range(30)]
               + ["arr%d%d" % (t, h) for t in range(NV) for h in range(NH)]
               + ["hop%d%d" % (t, h) for t in range(NV - 1) for h in range(NH)])
 
-PAR = {"g": 1.605, "s": 2.916, "pe": 0.569, "lat": 100.0, "far": 5700.0}
-KEYS = {"a0": -2.58, "g00": -2.41, "m0": 0.74, "a1": -0.03, "g01": 8.71, "m1": 3.7, "g10": 3.72, "e0": 9.16, "g11": 11.94, "e1": 8.51, "z0": 12.27}
-FV = set([(0, 0, 0, 1), (1, 0, 1, 2), (0, 1, 0, 1), (2, 0, 0, 1), (2, 0, 1, 2), (2, 1, 0, 1), (2, 1, 1, 2), (1, 0, 0, 1), (1, 1, 0, 1)])
-AHEAD = 0.002
-SOON = [450.0, 0.1]
-JIT = (792, 0.003)
+PAR = {"g": 1.56, "s": 3.5, "pe": 0.56, "lat": 250.0, "far": 5000.0, "first": 3000.0, "dma": 1800.0, "bw": 200.0,
+       "slow": 1.15, "run": 4, "tries": 50000, "warm": 200.0, "seed": 1}
+LONG = {"s": "f00 f00 a00 a00 a00 f01 f01 f02 f02 f02 a01 a01 a02 a02 a02 f10 f10 a10 f10 a10 a10 f11 f11 f12 a11 "
+             "f12 f12 a11 a12 a12 a12",
+        "v": "f00 d00 d00 d00 d01 d01 d02 d02 d02 d10 d10 d10 d11 d12 d11 d12 d12"}
 PLAN = {}
-ORDER = "7,0,1,2,3,57,52,59,51,5,6,8,11,10,53,12,50,33,13,36,14,46,47,48,34,58,18,16,22,17,76,19,23,21,20,9,28,44,15,37,24,25,26,38,129,62,72,39,27,73,49,63,45,85,87,88,128,41,89,35,86,90,74,96,118,117,98,99,97,64,75,65,4,93,91,30,92,94,29,43,100,111,108,116,95,66,67,68,69,70,60,71,61,103,119,104,101,105,126,102,40,127,106,120,109,42,107,110,112,113,114,121,77,122,123,54,84,146,133,130,147,31,148,151,141,124,149,125,134,131,115,150,152,153,154,138,132,135,160,155,161,162,156,214,142,157,158,143,163,173,164,139,137,140,174,32,136,144,165,166,78,167,170,168,171,169,175,215,222,172,178,81,179,181,218,80,180,219,216,176,145,182,177,185,232,192,183,184,243,225,220,186,217,193,187,194,205,195,188,223,189,226,196,190,197,198,199,202,200,221,206,224,227,228,203,201,207,210,159,253,79,204,55,211,256,229,212,230,83,213,191,233,254,257,208,234,284,252,260,240,241,308,261,242,82,235,56,247,263,309,209,244,270,245,248,246,231,249,264,255,262,258,259,236,265,266,237,267,250,251,268,271,269,273,238,293,278,272,281,239,274,275,288,276,289,294,282,283,285,339,338,279,286,295,287,290,296,280,297,277,299,298,291,292,306,307,300,303,301,304,302,318,310,326,305,313,314,311,321,322,319,327,328,329,315,312,323,320,330,333,331,334,332,348,317,316,324,356,335,357,343,340,359,358,361,325,360,363,364,351,362,370,336,344,341,365,371,372,373,374,345,342,347,346,383,366,349,367,350,368,352,353,384,354,369,375,376,377,380,378,379,385,381,388,425,435,337,389,382,391,390,428,426,355,424,392,395,386,402,393,394,432,396,427,403,436,397,404,398,399,429,453,405,415,462,406,387,400,416,433,430,442,431,437,434,438,407,408,409,417,410,411,420,421,412,422,413,466,423,439,414,440,418,443,467,518,470,471,463,419,464,444,450,451,452,480,494,473,519,454,445,457,455,458,456,441,472,468,465,446,469,459,460,461,474,401,447,475,476,448,477,449,478,483,481,484,482,498,479,503,485,488,489,491,492,549,504,486,493,505,499,495,548,496,497,500,506,490,507,508,501,502,509,487,516,510,517,511,513,512,514,520,536,531,523,515,524,525,528,521,532,522,529,538,537,533,530,539,540,543,526,534,527,535,541,544,542,545,558,553,566,561,550,567,554,569,568,562,570,571,573,572,580,546,551,563,574,575,581,576,582,577,583,584,559,593,634,552,578,555,556,585,586,560,594,547,587,579,588,590,589,564,557,635,638,598,645,565,591,599,592,601,600,603,602,605,604,636,639,612,642,637,607,595,596,597,606,608,613,614,609,615,616,625,610,640,646,647,626,641,643,617,644,618,619,622,620,627,623,621,648,679,708,652,663,630,631,687,680,683,690,649,624,611,628,650,688,653,651,684,689,681,691,655,632,656,685,654,682,686,692,629,657,667,633,673,658,660,693,661,697,694,662,695,698,668,664,665,674,659,666,675,700,699,705,706,676,707,709,677,678,669,710,712,670,671,711,713,714,718,696,701,702,719,703,704,720,721,715,722,716,723,672,717"
 
 
 def relay_of(src, dst, topo):
@@ -76,440 +81,474 @@ def mask_of(engines):
     return m
 
 
-def relay_program(g, core, T, topo, dst):
+def relay_program(g, core, T, topo, src, dst):
     eng = topo.engines(core, dst)
     rid, pid = topo.addr(dst, core)
     n = 0
     for t in range(NV - 1):
-        for h in range(NH):
-            c0 = 256 * t + CW * h
-            g.wait_ge(T.sem["hop%d%d" % (t, h)], len(eng))
-            g.remote_dma(T.w16[:, 256 + c0:256 + c0 + CW], T.wo[:, c0:c0 + CW], T.sem["arr%d%d" % (t, h)],
-                         T.sem.sent, pid, rid, mask_of(eng))
+        for h, (a, b) in enumerate(PARTS):
+            g.wait_ge(T.sem["hop%d%d" % (t, h)], len(topo.engines(src, core)))
+            g.remote_dma(T.w16[:, 256 * (t + 1) + a:256 * (t + 1) + b], T.wo[:, 256 * t + a:256 * t + b],
+                         T.sem["arr%d%d" % (t, h)], T.sem.sent, pid, rid, mask_of(eng))
             n += len(eng)
     g.wait_ge(T.sem.sent, n)
 
 
-def build(g, core, T, topo):
+def build(core, T, topo):
     ops = []
-    cur = [None]
     N = len(T.cores)
     rank = T.rank_of(core)
     nxt = T.cores[(rank + 1) % N]
     home = T.cores[(rank - (NV - 1)) % N]
     rel = relay_of(core, nxt, topo)
     eng_far = topo.engines(core, home)
+    tag = ["c"]
 
-    def op(e, cost, r, w, fn, bank=None, sem=None):
-        ops.append((e, cost, list(r), list(w), bank, fn, sem, cur[0]))
+    def R(name, a, b, step=1):
+        return (T[name][:, a:b:step] if step > 1 else T[name][:, a:b], name, a, b, len(range(a, b, step)), None)
 
-    def V(n, r, w, fn, bank=None):
-        op("v", max(64.0, n), r, w, fn, bank)
+    def R4(name, c0, c1, m=None, place=None):
+        t = T[name]
+        ap = t[:, c0:c1] if m is None and place is None else t[:, c0:c1, m, :] if place is None else t[:, c0:c1, :, place]
+        return (ap, name, 256 * c0, 256 * c1, (c1 - c0) * (256 if m is None and place is None else 16), None)
 
-    def S(n, r, w, fn, bank=None):
-        op("s", max(64.0, n), r, w, fn, bank)
+    def R3(name, c0, c1, s=None):
+        if s is None:
+            return (T[name][:, :, c0:c1], name, 0, 32, 2 * (c1 - c0), None)
+        return (T[name][:, s, c0:c1], name, 0, 32, c1 - c0, None)
 
-    def VG(n, r, w, fn, k="g"):
-        op("v", 60 + PAR[k] * n, r, w, fn)
+    def ind(win, off):
+        return (win[0].indirect(off[0]), win[1], win[2], win[3], 16 * off[4], off)
 
-    def SG(n, r, w, fn):
-        op("s", 78 + PAR["g"] * n, r, w, fn)
+    def mat(name):
+        k = 128 * MATS.index(name)
+        return R("mats", k, k + 128)
 
-    def P(bank, r, mm):
-        cost = 0.0
-        for m in mm:
-            cost += max(64, m[5]) * PAR["pe"] * (4 if len(m) > 6 else 1)
-        op("p", cost, r, [], lambda e: [e.matmul(m[0], m[1], m[2], m[3], m[4]) for m in mm], bank)
+    def band(name, m):
+        return R("bands", BANDS[name] + 16 - m, BANDS[name] + 144 - m)
 
-    def G(n, r, w, fn):
-        op("g", 150 + 2 * n, r, w, fn)
+    def col(k):
+        return R("cols", k, k + 1)
+
+    def ap(x):
+        return x[0] if isinstance(x, tuple) else x
+
+    def op(q, cost, reads, writes, fn, sem=None):
+        r = [x for x in reads if isinstance(x, tuple)]
+        r += [x[5] for x in r + writes if x[5]]
+        ops.append((q, cost, [x[1:4] for x in r], [x[1:4] for x in writes], fn, sem, tag[0]))
+
+    def short(*xs):
+        return all(SCRATCH[x[1]][2] in (bf, f16, u16) for x in xs)
+
+    def price(q, out, a, n):
+        if out[5]:
+            return (60, "s", out[4])
+        if a[5]:
+            return (60 if q == "v" else 78, "g", a[4])
+        return (max(64.0, n), "g", 0)
+
+    def TT(out, a, b, alu):
+        two = SCRATCH[a[1]][0] == SCRATCH[b[1]][0]
+        op("v", price("v", out, a, a[4] * (2 if two else 1)), [a, b], [out],
+           lambda e: e.tensor_tensor(out[0], a[0], b[0], alu))
+
+    def TS(out, a, s1, op0, s2=None, op1=None):
+        cost = price("v", out, a, a[4] * (0.5 if short(out, a) else 1))
+        if op1 is None:
+            op("v", cost, [a, s1], [out], lambda e: e.tensor_scalar(out[0], a[0], ap(s1), None, op0))
+        else:
+            op("v", cost, [a, s1, s2], [out], lambda e: e.tensor_scalar(out[0], a[0], ap(s1), ap(s2), op0, op1))
+
+    def CP(out, a):
+        op("v", price("v", out, a, a[4] * (0.5 if short(out, a) else 1)), [a], [out],
+           lambda e: e.tensor_copy(out[0], a[0]))
+
+    def SCAN(out, d0, d1, op0, op1):
+        op("v", (max(64, out[4]), "g", 0), [d0, d1], [out],
+           lambda e: e.tensor_tensor_scan(out[0], d0[0], d1[0], 0.0, op0, op1))
+
+    def SET(out, v):
+        op("v", (max(64.0, out[4] * (0.5 if short(out) else 1)), "g", 0), [], [out], lambda e: e.memset(out[0], v))
+
+    def ACT(out, a, func=F.Identity, bias=0.0, scale=1.0):
+        op("s", price("s", out, a, a[4]), [a, bias, scale], [out],
+           lambda e: e.activation(out[0], a[0], func, bias=ap(bias), scale=ap(scale)))
+
+    def EITHER(name, out, a, func=F.Identity, bias=0.0, scale=1.0):
+        if name not in ON_VECTOR.split():
+            ACT(out, a, func, bias, scale)
+        elif func == F.Sign:
+            TS(out, a, bias[6], A.is_gt, 2.0, A.mult)
+        elif func == F.Relu:
+            TS(out, a, bias, A.add, 0.0, A.max)
+        else:
+            TS(out, a, scale, A.mult, bias, A.add)
+
+    def MM(mm):
+        if len(mm) > PAR["run"]:
+            MM(mm[:PAR["run"]])
+            MM(mm[PAR["run"]:])
+            return
+        cost = sum(max(64, m[2][4]) * (4 if SCRATCH[m[1][1]][2] == f32 else 1) for m in mm)
+        op("p", (0, "pe", cost), [m[1] for m in mm] + [m[2] for m in mm], [m[0] for m in mm],
+           lambda e: [e.matmul(m[0][0], m[1][0], m[2][0], m[3], m[4]) for m in mm])
+
+    def IOTA(out, pattern, base, cm):
+        op("g", (160 + 2 * out[4], "g", 0), [], [out], lambda e: e.iota(out[0], pattern, base, cm))
+
+    def SEL(out, a, pattern, cmp, base, cm):
+        op("g", (205 + 2 * out[4], "g", 0), [a], [out],
+           lambda e: e.affine_select(out[0], a[0], pattern, cmp, 0.0, base, cm))
 
     nd = [0]
 
-    def D(nbytes, r, w, out, in_):
-        op("y", 2000 + nbytes / 180.0, r, w, lambda e: e.dma_start(out, in_), None, "d%d" % nd[0])
+    def DMA(out, a, size, after=None):
+        op("y", (PAR["dma"] + 128 * size * out[4] / PAR["bw"], "g", 0), [a, after], [out],
+           lambda e: e.dma_start(out[0], a[0]), "d%d" % nd[0])
         nd[0] += 1
 
-    mat_at = {}
+    def turned(buf, hbm, a, b, k, size, store=False):
+        here, there = R(buf, k * a, k * b), R(hbm, k * a, k * b)
+        DMA(*((there, here) if store else (here, there)), size)
 
-    def mat(name):
-        if name not in mat_at:
-            mat_at[name] = len(mat_at)
-        return T.mats[:, 128 * mat_at[name]:128 * mat_at[name] + 128]
+    turned("wi", "wd", *PARTS[0], 1, 4)
+    DMA(R("x0", 16, 2064), R("xt", 0, 2048), 2)
+    turned("wi", "wd", PARTS[0][1], 256, 1, 4)
+    DMA(R("x0", 2064, 2096), R("xt", 0, 32), 2)
+    DMA(R("wti", 0, 1), (T.wt[:], "wt", 0, 1, 1, None), 4)
+    DMA(R("pi", 0, 512), R("pd", 0, 512), 4, R("wi", 0, 1))
 
-    def B(name, h):
-        return T["%s%d" % (name, h)]
-
-    xw = [T.xa, T.xb]
-    xn = ["xa", "xb"]
-
-    def xres(b):
-        return [xn[b] + str(k) for k in range(NH)] + [xn[b] + "e"]
-
-    WN = ["wn%s%d" % (z, k) for z in "ab" for k in range(NH)]
-
-    D(131072, [], ["wi"], T.wi[:], T.wd[:])
-    D(524288, [], xres(0)[:NH], T.xa[:, 0:2048], T.xt[:])
-    D(8192, [], ["xae"], T.xa[:, 2048:2080], T.xt[:, 0:32])
-    D(512, [], ["wti"], T.wti[:, 0:1], T.wt[:])
-    D(262144, ["xa0"], ["pi"], T.pi[:], T.pd[:])
-
-    G(128, [], ["ia"], lambda e: e.iota(T.ia[:], [[-1, 128]], 128, 1))
-    G(128, [], ["ib"], lambda e: e.iota(T.ib[:], [[-16, 8], [0, 16]], 0, 1))
-    V(128, [], ["one32"], lambda e: e.memset(T.one32[:], 1.0))
-    G(128, ["one32"], ["i32m"], lambda e: e.affine_select(T.i32m[:], T.one32[:], [[-1, 128]], A.is_equal, 0.0, 0, 1))
-    G(160, [], ["ic"], lambda e: e.iota(T.ic[:], [[1, 160]], 0, -1))
-    G(CW, [], ["idd"], lambda e: e.iota(T.idd[:, 0:CW], [[256, NC], [1, 16]], -4096, 0))
-    G(16, [], ["ie"], lambda e: e.iota(T.ie[:], [[16, 16]], 0, 0))
-    V(128, ["ia"], ["ia"], lambda e: e.tensor_scalar(T.ia[:], T.ia[:], 15, None, A.bitwise_and))
-    V(128, ["ib"], ["ib"], lambda e: e.tensor_scalar(T.ib[:], T.ib[:], -16, None, A.bitwise_and))
-    V(256, ["ia", "ib"], ["rr"], lambda e: e.tensor_tensor(T.rr[:], T.ia[:], T.ib[:], A.add))
-    V(128, ["rr"], ["up"], lambda e: e.tensor_scalar(mat("up"), T.rr[:], 1.0, None, A.is_equal))
-    V(128, ["rr"], ["dn"], lambda e: e.tensor_scalar(mat("dn"), T.rr[:], 15.0, None, A.is_equal))
-    V(128, ["rr"], ["dn2"], lambda e: e.tensor_scalar(mat("dn2"), T.rr[:], 14.0, None, A.is_equal))
-    V(128, ["ib"], ["o"], lambda e: e.tensor_scalar(mat("o"), T.ib[:], 0.0, None, A.is_equal))
-
-    def scaled(name, src, rs, k):
-        S(128, [rs], [name], lambda e: e.activation(mat(name), src, F.Copy, scale=float(k)))
-
-    scaled("ni", T.i32m[:], "i32m", -1)
-    scaled("id", T.i32m[:], "i32m", 1)
-    scaled("n8k", T.i32m[:], "i32m", -8192)
-    scaled("ihi", T.i32m[:], "i32m", 3232)
-    scaled("ilo", T.i32m[:], "i32m", 2080)
-    scaled("uphi", mat("up"), "up", 3232)
-    scaled("uplo", mat("up"), "up", 2080)
-    scaled("ohi", mat("o"), "o", 1616)
-    scaled("olo", mat("o"), "o", 1040)
-    scaled("oh", mat("o"), "o", 0.5)
-    V(256, ["id", "up"], ["tm"], lambda e: e.tensor_tensor(mat("tm"), mat("id"), mat("up"), A.subtract))
-    V(256, ["dn2", "dn"], ["tq"], lambda e: e.tensor_tensor(mat("tq"), mat("dn2"), mat("dn"), A.subtract))
-    V(256, ["dn", "id"], ["tp"], lambda e: e.tensor_tensor(mat("tp"), mat("dn"), mat("id"), A.subtract))
-    S(128, ["tp"], ["sw32"], lambda e: e.activation(T.sw32[:], mat("tp"), F.Copy, scale=-0.5))
-    V(1, ["ia"], ["c0"], lambda e: e.tensor_copy(T.cols[:, 0:1], T.ia[:, 0:1]))
-    V(1, ["ia"], ["c1"], lambda e: e.tensor_scalar(T.cols[:, 1:2], T.ia[:, 0:1], 16.0, None, A.mult))
-    V(1, ["wti"], ["c3"], lambda e: e.tensor_copy(T.cols[:, 3:4], T.wti[:, 0:1]))
-    V(16, ["ia"], ["c16"], lambda e: e.tensor_scalar(T.cols[:, 16:32], T.ia[:, 0:16], 0.0, 2.0, A.is_equal, A.mult))
-    V(160, ["ic", "c0"], ["eb"], lambda e: e.tensor_scalar(T.eb[:], T.ic[:], T.cols[:, 0:1], 16.0, A.add, A.is_equal))
-    S(160, ["eb"], ["en"], lambda e: e.activation(T.en[:], T.eb[:], F.Copy, scale=-2048.0))
-    S(160, ["eb"], ["ep"], lambda e: e.activation(T.ep[:], T.eb[:], F.Copy, scale=4096.0))
-    S(160, ["eb", "c3"], ["ew"], lambda e: e.activation(T.ew[:], T.eb[:], F.Identity, scale=T.cols[:, 3:4]))
-    V(290, ["eb"], ["dbig"], lambda e: e.tensor_tensor(T.dbig[:, 1:145], T.eb[:, 2:146], T.eb[:, 0:144], A.subtract))
-
-    def esl(buf, m):
-        return buf[:, 16 - m:144 - m]
-
-    V(256, ["eb"], ["d0"], lambda e: e.tensor_tensor(mat("d0"), esl(T.eb, 15), esl(T.eb, 1), A.subtract))
-    V(256, ["eb"], ["d15"], lambda e: e.tensor_tensor(mat("d15"), esl(T.eb, 14), esl(T.eb, 0), A.subtract))
+    one, c8k = R("one", 0, 128), R("c8k", 0, 128)
+    SET(one, 1.0)
+    SEL(mat("id"), one, [[-1, 128]], A.is_equal, 0, 1)
+    SEL(mat("up"), one, [[-1, 128]], A.is_equal, -1, 1)
+    k0 = 128 * MATS.index("up")
+    SEL(R("mats", k0 + 15, k0 + 128, 16), R("one", 0, 8), [[-16, 8]], A.is_equal, 0, 1)
+    for k, v in enumerate((2080.0, 3232.0)):
+        SET(R("cs", 128 * k, 128 * k + 128), v)
+    an, aq = R("acol", 0, 1), R("acol", 1, 2)
+    SET(an, 16.0)
+    SET(aq, 0.0)
+    for x in ("x0", "x1"):
+        SET(R(x, 0, 16), 0.0)
+    for name, src, k in (("ihi", "id", 3232), ("ilo", "id", 2080), ("uphi", "up", 3232), ("uplo", "up", 2080),
+                         ("ni", "id", -1)):
+        ACT(mat(name), mat(src), scale=float(k))
+    for a, b in PARTS:
+        TS(R("w16", a, b), R("wi", a, b), -2048.0, A.add)
+    SEL(mat("o"), one, [[-16, 8], [0, 16]], A.is_ge, 0, 1)
+    SEL(mat("o"), mat("o"), [[16, 8], [0, 16]], A.is_ge, 15, -1)
+    for name, k in (("ohi", 3232), ("olo", 2080)):
+        ACT(mat(name), mat("o"), scale=float(k))
+    IOTA(R("ia", 0, 16), [[-1, 16]], 128, 1)
+    TS(R("ia", 0, 16), R("ia", 0, 16), 15, A.bitwise_and)
+    CP(col(0), R("ia", 0, 1))
+    ACT(col(1), col(0), scale=16.0)
+    CP(col(2), R("wti", 0, 1))
+    TS(R("cols", 16, 32), R("ia", 0, 16), 0.0, A.is_equal)
+    ACT(col(3), col(16), scale=K, bias=-4096.0)
+    TS(col(4), col(17), col(16), A.subtract, 4096.0, A.mult)
+    ACT(col(5), col(0), scale=-K, bias=-0.5)
+    ACT(col(6), col(0), scale=-K, bias=-4096.0)
+    ACT(col(7), col(16), scale=-K)
+    ACT(col(8), col(0), scale=K)
+    ACT(col(9), col(0), scale=K, bias=0.5)
+    ACT(col(10), col(0), scale=K, bias=4096.0)
+    SET(R("bands", 0, 896), 0.0)
+    k0 = 128 * MATS.index("o")
+    o8 = R("mats", k0, k0 + 128, 16)
+    for name, at, k in (("en", 16, -2048.0), ("ep", 16, 4096.0), ("ew", 16, col(2)), ("dd", 15, 1.0), ("dd", 17, -1.0),
+                        ("d0", 15, 1.0), ("d0", 1, -1.0), ("d15", 14, 1.0), ("d15", 0, -1.0)):
+        ACT(R("bands", BANDS[name] + at, BANDS[name] + at + 113, 16), o8, scale=k)
 
     def dk(k):
-        return mat("d0") if k == 0 else mat("d15") if k == 15 else esl(T.dbig, k)
+        if k in (0, 15):
+            return R("bands", BANDS["d%d" % k], BANDS["d%d" % k] + 128)
+        return band("dd", k)
 
-    V(CW, ["idd", "c1"], ["ck"], lambda e: e.tensor_scalar(T.ck[:], T.idd[:, 0:CW], T.cols[:, 1:2], None, A.add))
-    V(CW, ["ck"], ["cke"], lambda e: e.tensor_scalar(T.cke[:], T.ck[:], -4096.0 * 4080, None, A.add))
-    for a, v in enumerate((15, 1, 0, 0)):
-        S(CW, ["one32", "c16"], ["coh%d" % a], lambda e, a=a, v=v: e.activation(
-            T.coh[:, CW * a:CW * a + CW], T.one32[:, 0:CW], F.Identity, scale=T.cols[:, 16 + v:17 + v]))
-    V(64, [], ["cac0"], lambda e: e.memset(T.cac[:, 0:CW], 2080.0))
-    V(64, [], ["cac1"], lambda e: e.memset(T.cac[:, CW:2 * CW], 3232.0))
-    V(CW, [], ["msk"], lambda e: e.memset(T.msk[:], 1.0))
-    V(NC, [], ["msk"], lambda e: e.memset(T.msk[:, 0:CW:16], 0.0))
-    V(512, [], WN, lambda e: e.memset(T.wn[:], 0.0))
-    V(64, [], ["oneb"], lambda e: e.memset(T.oneb[:], 1.0))
-    V(1, [], ["gdc"], lambda e: e.memset(T.gd[:, 16:17], 31.0 / 256))
-    V(1, [], ["acol"], lambda e: e.memset(T.acol[:, 0:1], 0.0))
-    if EXP:
-        G(CW, [], ["ig"], lambda e: e.iota(T.ig[:, 0:CW], [[16, CW]], 0, 0))
-        V(CW, ["ig", "c0"], ["cz"], lambda e: e.tensor_scalar(T.cz[:], T.ig[:, 0:CW], T.cols[:, 0:1], None, A.add))
-        V(CW, ["ia"], ["dia"], lambda e: e.tensor_scalar(T.dia[:], T.ia[:, 0:CW], 0.0, None, A.is_equal))
-        V(16, ["ie"], ["lc"], lambda e: e.tensor_scalar(T.lc[:], T.ie[:], 1.0 / 16, None, A.mult))
-        scaled("o8k", mat("o"), "o", 8192)
-    else:
-        V(CW, ["one32", "c0"], ["cz"], lambda e: e.tensor_scalar(T.cz[:], T.one32[:, 0:CW], T.cols[:, 0:1], None, A.mult))
-        V(64, [], ["c8k"], lambda e: e.memset(T.c8k[:], 8192.0))
-        for m in range(16):
-            G(128, ["c8k"], ["rm%d" % m], lambda e, m=m: e.affine_select(
-                T.rm[:, 128 * m:128 * m + 128], T.c8k[:], [[-16, 8], [0, 16]], A.is_equal, 0.0, -m, 1))
-    V(16, ["ie", "c0"], ["ti"], lambda e: e.tensor_scalar(T.ti[:], T.ie[:], T.cols[:, 0:1], None, A.add))
-    if not EXP:
-        V(16, ["ti"], ["b16"], lambda e: e.tensor_scalar(T.b16[:], T.ti[:], 16.0, None, A.mult))
-    V(16, ["ti"], ["ct"], lambda e: e.tensor_scalar(T.ct[:], T.ti[:], 32.0, -2048.0 * 8164 - 1024, A.mult, A.add))
-    for h in range(NH):
-        V(16, ["ti"], ["cb%d" % h], lambda e, h=h: e.tensor_scalar(
-            T.cb[:, NC * h:NC * h + NC], T.ti[:, 0:NC], 8.0, None, A.mult))
-    V(16, ["ti"], ["cbd"], lambda e: e.tensor_scalar(T.cb[:, 16:32], T.ti[:], -512.0, None, A.add))
-    V(16, ["ti"], ["t256"], lambda e: e.tensor_scalar(T.t256[:], T.ti[:], 1.0 / 256, 1.0, A.mult, A.add))
-    V(16, ["ti"], ["lsb"], lambda e: e.tensor_scalar(T.lsb[:], T.ti[:], 512.0, None, A.add))
-    V(512, ["pi"], ["sw"], lambda e: e.tensor_scalar(T.sw[:, 0:512], T.pi[:], -2048.0, None, A.add))
-    for h in range(NH):
-        V(CW, ["wi"], ["w0%d" % h], lambda e, h=h: e.tensor_scalar(
-            T.w16[:, CW * h:CW * h + CW], T.wi[:, CW * h:CW * h + CW], -2048.0, None, A.add))
+    IOTA(R("ic", 0, 128), [[256, 8], [1, 16]], 0, 0)
+    SET(R("ck", 0, 128), 0.0)
+    TS(R("ck", 128, 256), R("ic", 0, 128), col(1), A.add)
+    SET(R("msk", 0, 128), 0.0)
+    SET(R("msk", 0, 128, 16), 2.0 ** 25)
+    SET(c8k, K)
+    for m in range(16):
+        SEL(R("rm", 128 * m, 128 * m + 128), c8k, [[-16, 8], [0, 16]], A.is_equal, -m, 1)
+    q0, q1, q2, q3 = [R("ps%d" % COUNT, 128 * k, 128 * k + 128) for k in range(4)]
+    MM([(q0, mat("id"), mat("up"), True, False), (q0, mat("id"), mat("ni"), False, True),
+        (q1, mat("up"), mat("id"), True, False), (q1, mat("id"), mat("ni"), False, True)])
+    ACT(mat("tp2"), q1)
+    ACT(mat("um"), q0)
+    ACT(mat("tm"), q0, scale=-0.5)
+    ACT(mat("tpk"), q1, scale=K / 2)
+    ACT(R("imd", 0, 128), q1, scale=-1.0)
+    MM([(q2, mat("up"), mat("tp2"), True, True),
+        (q3, mat("up"), mat("tp2"), True, False), (q3, mat("ni"), mat("tp2"), False, True)])
+    ACT(mat("tq"), q2, scale=0.5)
+    ACT(mat("sk"), q3, scale=2048.0)
+    ACT(R("coh", 0, 128), one, scale=col(31))
+    ACT(R("coh", 128, 256), one, scale=col(17))
+    ACT(R("cm", 0, 128), c8k, scale=col(16), bias=-2 * K)
+    ACT(R("cm", 128, 256), c8k, scale=col(16), bias=2048 - 2 * K)
+    for a in (0, 256):
+        ACT(R("bz", a, a + 256, 2), one, scale=0.0)
+    for a, b in PARTS:
+        IOTA(R("ie", a // 16, b // 16), [[16, (b - a) // 16]], 0, 0)
+    IOTA(R("ie", 16, 32), [[16, 16]], 0, 0)
+    TS(R("tl", 0, 16), R("ie", 0, 16), col(0), A.add)
+    TS(R3("sc", 0, 16, 0), R("ie", 16, 32), col(0), A.add, 2.0, A.mult)
+    ACT(R3("sc", 0, 16, 1), R3("sc", 0, 16, 0), bias=1.0)
+    for s in range(2):
+        ACT(R3("sx", 0, 16, s), R("tl", 0, 16), scale=0.0, bias=512.0 - s)
+    for name, k, c in (("b16", 16, 0), ("ct", 32, -1000), ("cb", 8, 0), ("t2", 2, 1)):
+        ACT(R(name, 0, 16), R("tl", 0, 16), scale=float(k), bias=float(c))
+    SET(R("gd", 16, 17), -16.25 / 128)
+    for a in (0, 256):
+        TS(R("sw0", a, a + 256), R("pi", a, a + 256), -2048.0, A.add)
 
-    def finish_lists(h, st):
-        p1, b1, xi, p32 = B("ps%d" % h, 1), "p%d1" % h, B("xi", h), B("p32", h)
-        for z, c in (("a", 0), ("b", CW)):
-            pz, c2 = ("a", 0) if st == 0 else (z, c)
-            k = "xi%s%d" % (z, h)
-            V(CW, ["p32%s%d" % (pz, h)], [k], lambda e, c=c, c2=c2: e.tensor_tensor(
-                xi[:, c:c + CW], p1[:, c:c + CW], p32[:, c2:c2 + CW], A.add), b1)
-            V(CW, [k], [k], lambda e, c=c: e.tensor_scalar(
-                xi[:, c:c + CW], xi[:, c:c + CW], 5, 2047, A.arith_shift_right, A.bitwise_and))
-            V(CW, ["acol", k], ["off%s%d" % (z, h)], lambda e, c=c: e.tensor_scalar(
-                B("off", h)[:, c:c + CW], xi[:, c:c + CW], T.acol[:, 0:1], None, A.add))
+    def sizes(h):
+        i0, i1 = PARTS[h]
+        return i0, i1, i1 - i0, i0 // 16, i1 // 16
+
+    def at(h, what, a=0, b=1, step=1):
+        n = PARTS[h][1] - PARTS[h][0]
+        bank = BANKS[h]["SKDOI".index(what) - 1 if what != "S" else 0]
+        base = n if what == "K" else 0
+        if what in "OI" and BANKS[h][1] == bank:
+            base = n
+        return R("ps%d" % bank, base + int(a * n), base + int(b * n), step)
+
+    def lists(h, st):
+        i0, i1, n, c0, c1 = sizes(h)
+        for a, b in ((0, n), (n, 2 * n)) if (st, h) in SPLIT else ((0, 2 * n),):
+            xi = R("xi%d" % h, a, b)
+            TS(xi, R("xj%d" % h, 2 * a + 1, 2 * b, 2) if st else xi, 5, A.arith_shift_right, 2047, A.bitwise_and)
+            TS(R("off%d" % h, a, b), xi, an, A.add, aq, A.subtract)
 
     def gathers(t, st, h):
-        x = xw[t % 2]
-        ph = "g%d%d" % (st, h)
-        cur[0] = (t, ph)
-        p2, p3 = B("ps%d" % h, 2), B("ps%d" % h, 3)
-        P("p%d2" % h, ["i32m", "ck", "cke"], [(p2[:, 0:CW], T.i32m[:], (T.cke if st else T.ck)[:], True, False, CW, 4)])
-        if st == 0:
-            P("p%d3" % h, ["n8k", "cz"], [(p3[:, 0:CW], mat("n8k"), T.cz[:], True, False, CW)])
-        for s in range(NS):
-            cur[0] = (t, ph, 0.01 * s - AHEAD)
-            a, b = 16 * SW * s, 16 * SW * (s + 1)
-            fb, db, ab, off = B("fb", h)[:, a:b], B("db", h)[:, a:b], B("ab", h), B("off", h)
-            o1, o2 = off[:, SW * s:SW * s + SW], off[:, CW + SW * s:CW + SW * s + SW]
-            k = "%d%d" % (h, s)
-            if (t, st, h, s) in FV:
-                VG(b - a, xres(t % 2) + ["offa%d" % h], ["fb" + k], lambda e, fb=fb, o1=o1: e.tensor_copy(fb, x[:].indirect(o1)))
+        i0, i1, n, c0, c1 = sizes(h)
+        x = R("x%d" % (t % 2), 0, 2096)
+        fb, db, ab, off = [s + str(h) for s in ("fb", "db", "ab", "off")]
+        tag[0] = "%d g%d%d" % (t, st, h)
+        Kb, Db = at(h, "K")[1], at(h, "D")[1]
+        MM([(at(h, "K"), mat("id"), R("ck", 128, 128 + n), True, False)])
+        once = PIECES[st, h].count("+") == len(PIECES[st, h].split()) - 1
+        if st == 0 and not once:
+            MM([(at(h, "D"), mat("id"), R("ck", 0, n), True, False)])
+        a = first = 0
+        for word in PIECES[st, h].split():
+            b = a + int(word.rstrip("aA+"))
+            f, o1, o2 = R(fb, 16 * a, 16 * b), R(off, a, b), R(off, n + a, n + b)
+            if "A" in word:
+                CP(f, ind(x, o1))
             else:
-                SG(b - a, xres(t % 2) + ["offa%d" % h], ["fb" + k],
-                   lambda e, fb=fb, o1=o1: e.activation(fb, x[:].indirect(o1), F.Copy))
-            VG(b - a, xres(t % 2) + ["offb%d" % h, "fb" + k], ["db" + k],
-               lambda e, fb=fb, db=db, o2=o2: e.tensor_tensor(db, x[:].indirect(o2), fb, A.subtract))
-            cur[0] = (t, ph, 0.01 * s - 0.005)
-            c0, c1 = SW // 16 * s, SW // 16 * (s + 1)
-            S(b - a, ["db" + k], ["ab" + k], lambda e, db=db, c0=c0, c1=c1: e.activation(ab[:, c0:c1], db, F.Abs))
-            if (s + 1) % NP:
+                ACT(f, ind(x, o1), F.Copy)
+            TT(R(db, 16 * a, 16 * b), ind(x, o2), f, A.subtract)
+            ACT(R4(ab, a // 16, b // 16), R(db, 16 * a, 16 * b), F.Abs)
+            a = b
+            if word.endswith("+"):
                 continue
-            c0 = c1 - NP * SW // 16
-            AB = ["ab%d%d" % (h, z) for z in range(s + 1 - NP, s + 1)]
-            P("p%d2" % h, AB + ["en", "ep"],
-              [(p2[:, 16 * c0:16 * c1], esl(T.ep if st else T.en, m), ab[:, c0:c1, m, :], False,
-                s == NS - 1 and m == 15, NP * SW) for m in range(16)])
+            MM([(R(Kb, n + first, n + b), band("ep" if st else "en", m), R4(ab, first // 16, b // 16, m=m), False,
+                 b == n and m == 15) for m in range(16)])
             if st == 0:
-                P("p%d3" % h, AB + ["dbig", "d0", "d15"],
-                  [(p3[:, 16 * c0:16 * c1], dk(m), ab[:, c0:c1, :, m], False, False, NP * SW) for m in range(16)])
+                MM([(R(Db, first, b), dk(m), R4(ab, first // 16, b // 16, place=m), once and m == 0, False)
+                    for m in range(16)])
+            first = b
+        assert a == n
 
-    def pick(h, first):
-        p2, p3, rs, ix, kb = B("ps%d" % h, 2), B("ps%d" % h, 3), B("rs", h), B("ix", h), B("kb", h)
-        hs = str(h)
-        V(CW, ["msk"], ["rs" + hs], lambda e: e.tensor_tensor_scan(rs[:], T.msk[:], p2[:, 0:CW], 0.0, A.mult, A.min), "p%d2" % h)
-        V(NC, ["rs" + hs], ["ix" + hs], lambda e: e.tensor_scalar(ix[:, 0:NC], rs[:, 15:CW:16], 2047, None, A.bitwise_and))
-        V(NC, ["ix" + hs], ["lk" + hs], lambda e: e.tensor_copy(B("lk", h)[:, 0:NC], ix[:, 0:NC]))
-        if first:
-            P("p%d3" % h, ["n8k", "cz"], [(p3[:, 0:CW], mat("n8k"), T.cz[:], True, False, CW)])
-        if EXP:
-            VG(CW, ["ix" + hs, "lc", "dia"], ["kb" + hs], lambda e: e.tensor_tensor(
-                kb[:], ix[:, 0:NC].indirect(T.lc[:, 0:NC]), T.dia[:], A.mult))
-            P("p%d3" % h, ["kb" + hs, "o8k"], [(p3[:, 0:CW], mat("o8k"), kb[:], False, True, CW)])
-        else:
-            V(NC, ["ix" + hs, "b16"], ["kb" + hs], lambda e: e.tensor_tensor(kb[:, 0:NC], ix[:, 0:NC], T.b16[:, 0:NC], A.subtract))
-            P("p%d3" % h, ["kb" + hs] + ["rm%d" % m for m in range(16)],
-              [(p3[:, m:CW:16], T.rm[:, 128 * m:128 * m + 128], kb[:, 0:NC], False, m == 15, NC) for m in range(16)])
-
-    FB = lambda h: ["fb%d%d" % (h, s) for s in range(NS)]
-    DB = lambda h: ["db%d%d" % (h, s) for s in range(NS)]
+    def pick(h, st):
+        i0, i1, n, c0, c1 = sizes(h)
+        SCAN(R("rs", i0, i1), R("msk", 0, n), at(h, "K"), A.add, A.min)
+        TS(R("ix", c0, c1), R("rs", i0 + 15, i1, 16), 2047, A.bitwise_and)
+        TT(R("kb", c0, c1), R("ix", c0, c1), R("b16", c0, c1), A.subtract)
+        CP(R("lk", c0, c1), R("ix", c0, c1))
+        if st:
+            MM([(at(h, "S"), mat("id"), R("ck", 0, n), True, False)])
+        MM([(R(at(h, "S" if st else "D")[1], m, n, 16), R("rm", 128 * m, 128 * m + 128), R("kb", c0, c1), False,
+             m == 15) for m in range(16)])
 
     def stage1(t, h):
-        w, wr = T.w16[:, 256 * t + CW * h:256 * t + CW * h + CW], "w%d%d" % (t, h)
-        p0, p1 = B("ps%d" % h, 0), B("ps%d" % h, 1)
-        b0, b1 = "p%d0" % h, "p%d1" % h
-        cur[0] = (t, "a%d" % h, -0.001)
-        P(b0, [wr, "up"], [(p0[:, 0:CW], mat("up"), w, True, True, CW)])
-        cur[0] = (t, "a%d" % h)
-        P(b1, [wr, "ihi", "ilo", "uphi", "uplo"],
-          [(p1[:, 0:CW], mat("ihi"), w, True, False, CW), (p1[:, 0:CW], mat("uplo"), w, False, True, CW),
-           (p1[:, CW:2 * CW], mat("ilo"), w, True, False, CW), (p1[:, CW:2 * CW], mat("uphi"), w, False, True, CW)])
-        V(CW, [wr], ["p32a%d" % h], lambda e: e.tensor_tensor(B("p32", h)[:, 0:CW], p0[:, 0:CW], w, A.mult), b0)
-        finish_lists(h, 0)
-        P(b0, [wr, "up", "ni"],
-          [(p0[:, CW:2 * CW], mat("up"), w, True, False, CW), (p0[:, CW:2 * CW], mat("ni"), w, False, True, CW)])
-        S(CW, [], ["dw%d" % h], lambda e: e.activation(B("dw", h)[:], p0[:, CW:2 * CW], F.Copy), b0)
+        i0, i1, n, c0, c1 = sizes(h)
+        w, p32 = R("w16", 256 * t + i0, 256 * t + i1), R("p32%d" % h, 0, n)
+        Ia, Ib, Ic = [at(h, "I", k, k + 1) for k in range(3)]
+        tag[0] = "%d a%d" % (t, h)
+        MM([(Ia, mat("up"), w, True, True), (Ib, mat("ihi"), w, True, False), (Ib, mat("uplo"), w, False, True)])
+        MM([(Ic, mat("ilo"), w, True, False), (Ic, mat("uphi"), w, False, True)])
+        TT(p32, Ia, w, A.mult)
+        TT(R("xi%d" % h, 0, n), Ib, p32, A.add)
+        TT(R("xi%d" % h, n, 2 * n), Ic, p32, A.add)
+        lists(h, 0)
         gathers(t, 0, h)
 
     def middle(t, h):
-        w, wr = T.w16[:, 256 * t + CW * h:256 * t + CW * h + CW], "w%d%d" % (t, h)
-        p0, p1, p2, p3 = [B("ps%d" % h, b) for b in range(4)]
-        b0, b1, b2, b3 = ["p%d%d" % (h, b) for b in range(4)]
-        gg, tt, p32, b32 = B("gg", h), B("tt", h), B("p32", h), B("b32", h)
-        hs = str(h)
-        pick(h, False)
-        SG(CW, FB(h) + ["lk" + hs], ["fk" + hs], lambda e: e.activation(
-            B("fk", h)[:], B("fb", h)[:].indirect(B("lk", h)[:, 0:NC]), F.Copy))
-        P(b2, ["fk" + hs, "ew"], [(p2[:, CW:CW + NC], esl(T.ew, m), B("fk", h)[:, m:CW:16], m == 0, m == 15, NC)
-                                  for m in range(16)])
-        S(CW, [], ["ga" + hs], lambda e: e.activation(gg[:, 0:CW], p3[:, 0:CW], F.Sign, bias=-0.5), b3)
-        S(CW, [], ["gb" + hs], lambda e: e.activation(gg[:, CW:2 * CW], p3[:, 0:CW], F.Sign, bias=-4096.0), b3)
-        ui = T.ui[:, NC * h:NC * h + NC]
-        V(NC, [], ["ui" + hs], lambda e: e.tensor_copy(ui, p2[:, CW:CW + NC]), b2)
-        V(NC, ["ui" + hs], ["u9" + hs], lambda e: e.tensor_scalar(B("u9", h)[:, 0:NC], ui, 511, None, A.bitwise_and))
-        V(NC, ["u9" + hs], ["lb" + hs], lambda e: e.tensor_copy(B("lb", h)[:, 0:NC], B("u9", h)[:, 0:NC]))
-        SG(CW, ["sw", "lb" + hs], ["b32" + hs], lambda e: e.activation(
-            b32[:], T.sw[:, 0:512].indirect(B("lb", h)[:, 0:NC]), F.Copy))
-        V(NC, ["rs" + hs, "ct"], ["th" + hs], lambda e: e.tensor_tensor(
-            B("th", h)[:, 0:NC], T.ct[:, 0:NC], B("rs", h)[:, 15:CW:16], A.subtract))
-        P(b0, ["ga" + hs, "id", "tm", "tq", "coh0", "coh1"],
-          [(p0[:, 0:2 * CW], mat("id"), T.coh[:, 0:2 * CW], True, False, 2 * CW),
-           (p0[:, 0:CW], mat("tm"), gg[:, 0:CW], False, False, CW),
-           (p0[:, CW:2 * CW], mat("tq"), gg[:, 0:CW], False, True, CW)])
-        V(CW, [wr], ["ta" + hs], lambda e: e.tensor_tensor(tt[:, 0:CW], p0[:, 0:CW], w, A.mult), b0)
-        V(CW, [wr], ["tb" + hs], lambda e: e.tensor_tensor(tt[:, CW:2 * CW], p0[:, CW:2 * CW], w, A.mult), b0)
-        P(b1, ["ta" + hs, "tb" + hs, "id", "cac0", "cac1", "oh"],
-          [(p1[:, 2 * CW:4 * CW], mat("id"), T.cac[:], True, False, 2 * CW),
-           (p1[:, 2 * CW:4 * CW], mat("oh"), tt[:], False, True, 2 * CW)])
-        P(b1, ["ta" + hs, "tb" + hs, "ohi", "olo"],
-          [(p1[:, 0:CW], mat("ohi"), tt[:, 0:CW], True, True, CW),
-           (p1[:, CW:2 * CW], mat("olo"), tt[:, CW:2 * CW], True, True, CW)])
-        V(CW, ["b32" + hs], ["p32a" + hs], lambda e: e.tensor_tensor(p32[:, 0:CW], p1[:, 2 * CW:3 * CW], b32[:], A.mult), b1)
-        V(CW, ["b32" + hs], ["p32b" + hs], lambda e: e.tensor_tensor(p32[:, CW:2 * CW], p1[:, 3 * CW:4 * CW], b32[:], A.mult), b1)
-        finish_lists(h, 1)
-        P(b0, ["ga" + hs, "gb" + hs, "id", "tp", "coh2", "coh3"],
-          [(p0[:, 2 * CW:4 * CW], mat("id"), T.coh[:, 2 * CW:4 * CW], True, False, 2 * CW),
-           (p0[:, 2 * CW:4 * CW], mat("tp"), gg[:], False, True, 2 * CW)])
-        S(CW, [], ["ohp" + hs], lambda e: e.activation(B("ohp", h)[:], p0[:, 2 * CW:3 * CW], F.Copy, scale=0.5), b0)
-        V(CW, ["dw" + hs], ["s32" + hs], lambda e: e.tensor_tensor(
-            B("s32", h)[:], p0[:, 3 * CW:4 * CW], B("dw", h)[:], A.mult), b0)
-        P(b3, ["s32" + hs, wr, "id", "sw32"],
-          [(p3[:, 3 * CW:4 * CW], mat("id"), w, True, False, CW),
-           (p3[:, 3 * CW:4 * CW], T.sw32[:], B("s32", h)[:], False, True, CW, 4)])
-        S(CW, [], ["wnb" + hs], lambda e: e.activation(
-            T.wn[:, 256 + CW * h:256 + CW * h + CW], p3[:, 3 * CW:4 * CW], F.Copy), b3)
+        i0, i1, n, c0, c1 = sizes(h)
+        w, sw, tt = R("w16", 256 * t + i0, 256 * t + i1), "sw%d" % (t % 2), "tt%d" % h
+        ga, gb, r1 = [R(s, i0, i1) for s in ("ga", "gb", "r1")]
+        Oa, Ob, Oc, Od = [at(h, "O", k, k + 1) for k in range(4)]
+        I, e0 = at(h, "I")[1:3]
+        even = R(I, e0, e0 + 4 * n, 2)
+        u = R(at(h, "S")[1], 0, c1 - c0)
+        tag[0] = "%d m%d" % (t, h)
+        o_start = [(at(h, "O", 0, 2), mat("id"), R("coh", 128 - n, 128 + n), True, False)]
+        i_start = [(even, mat("id"), R("cs", 128 - n, 128 + n), True, False)]
+        if BANKS[h][2] != BANKS[h][1]:
+            MM(o_start)
+            o_start = []
+        if BANKS[h][3] not in BANKS[h][1:3]:
+            MM(i_start)
+            i_start = []
+        pick(h, 0)
+        EITHER("fk%d" % h, R("fk", i0, i1), ind(R("fb%d" % h, 0, 16 * n), R("lk", c0, c1)))
+        MM([(u, band("ew", m), R("fk", i0 + m, i1, 16), m == 0, m == 15) for m in range(16)])
+        CP(R("ui", c0, c1), u)
+        EITHER("ga%d" % h, ga, at(h, "D"), F.Sign, bias=col(5) + (col(9),))
+        TS(R("u9", c0, c1), R("ui", c0, c1), 511, A.bitwise_and)
+        CP(R("lb", c0, c1), R("u9", c0, c1))
+        EITHER("bz%d" % h, R("bz", 2 * i0 + 1, 2 * i1, 2), ind(R(sw, 0, 512), R("lb", c0, c1)))
+        TT(R("th", c0, c1), R("ct", c0, c1), R("rs", i0 + 15, i1, 16), A.subtract)
+        MM(o_start + [(Oa, mat("tm"), ga, False, False), (Ob, mat("tq"), ga, False, True)])
+        TT(R(tt, 0, n), Oa, w, A.mult)
+        TT(R(tt, n, 2 * n), Ob, w, A.mult)
+        MM(i_start + [(even, mat("o"), R(tt, 0, 2 * n), False, True),
+                      (R(I, e0 + 1, e0 + 2 * n, 2), mat("ohi"), R(tt, 0, n), True, True),
+                      (R(I, e0 + 2 * n + 1, e0 + 4 * n, 2), mat("olo"), R(tt, n, 2 * n), True, True)])
+        for k in range(2):
+            SCAN(R("xj%d" % h, 2 * k * n, 2 * k * n + 2 * n), R("bz", 2 * i0, 2 * i1), at(h, "I", 2 * k, 2 * k + 2),
+                 A.mult, A.add)
+        lists(h, 1)
+        tag[0] = "%d x%d" % (t, h)
+        EITHER("gb%d" % h, gb, at(h, "D"), F.Sign, bias=col(6) + (col(10),))
+        MM([(Ob, mat("um"), w, True, False), (Ob, mat("tpk"), gb, False, True)])
+        EITHER("r%d" % h, r1, Ob, F.Relu, bias=col(3))
+        MM([(Oc, mat("id"), w, True, False), (Oc, mat("sk"), gb, False, False), (Oc, R("imd", 0, 128), r1, False, True)])
+        MM([(Od, mat("tpk"), ga, True, False), (Od, mat("ni"), w, False, True)])
+        EITHER("sw%d" % h, R(sw, 512 + 2 * i0 + 1, 512 + 2 * i1, 2), Oc, bias=col(4))
+        EITHER("sw%d" % h, R(sw, 512 + 2 * i0, 512 + 2 * i1, 2), Od, scale=-1.0, bias=col(7))
+        cm = 128 if t == NV - 1 else 0
+        MM([(Oa, mat("id"), R("cm", cm, cm + n), True, False), (Oa, mat("tpk"), ga, False, False)])
 
-    def write_lists():
-        UI = ["ui%d" % h for h in range(NH)]
-        V(16, UI, ["sma"], lambda e: e.tensor_scalar(T.sm[:, 0:16], T.ui[:], 7, None, A.bitwise_and))
-        V(16, UI, ["smb"], lambda e: e.tensor_scalar(T.sm[:, 16:32], T.ui[:], 1, None, A.bitwise_and))
-        V(32, ["sma", "smb", "cbd"] + ["cb%d" % h for h in range(NH)], ["sm2"],
-          lambda e: e.tensor_tensor(T.sm2[:], T.sm[:], T.cb[:], A.add))
-        V(16, ["sm2"], ["lx"], lambda e: e.tensor_copy(T.lx[:], T.sm2[:, 0:16]))
+    def write_lists(t):
+        tag[0] = "%d l" % t
+        TS(R("sm", 0, 16), R("ui", 0, 16), 7, A.bitwise_and)
+        TT(R("sm2", 0, 16), R("sm", 0, 16), R("cb", 0, 16), A.add)
+        CP(R("lx", 0, 16), R("sm2", 0, 16))
+        TS(R("sm", 16, 32), R("ui", 0, 16), 1, A.bitwise_and)
 
-    def write_stock(t, hh):
-        a, b = NC * hh[0], NC * (hh[-1] + 1)
-        k = str(hh[0])
-        V(16, ["gd%d" % h for h in hh] + ["sm2"], ["g6" + k], lambda e: e.tensor_tensor(
-            T.g6[:, a:b], T.gd[:, a:b], T.sm2[:, 16 + a:16 + b], A.mult))
-        V(16, ["g6" + k, "lsb"], ["g6" + k], lambda e: e.tensor_tensor(T.g6[:, a:b], T.g6[:, a:b], T.lsb[:, a:b], A.add))
-        V(16, ["g6" + k], ["ls" + k], lambda e: e.tensor_copy(T.ls[:, a:b], T.g6[:, a:b]))
-        VG(16 * (b - a), ["wna%d" % h for h in hh] + ["ls" + k], ["sw"],
-           lambda e: e.tensor_copy(T.sw[:].indirect(T.ls[:, a:b]), T.wn[:, 16 * a:16 * b]), "s")
+    def write_stock(t, i0, i1):
+        c0, c1 = i0 // 16, i1 // 16
+        tag[0] = "%d z" % t
+        TT(R3("hh", c0, c1, 1), R("gd", c0, c1), R("sm", 16 + c0, 16 + c1), A.mult)
+        TT(R3("hh", c0, c1, 0), R("gd", c0, c1), R3("hh", c0, c1, 1), A.subtract)
+        TT(R3("hh", c0, c1), R3("hh", c0, c1), R3("sx", c0, c1), A.mult)
+        TT(R3("hh", c0, c1), R3("hh", c0, c1), R3("sc", c0, c1), A.add)
+        CP(R3("ls", c0, c1), R3("hh", c0, c1))
+        for s in range(2):
+            src = ind(R("sw%d" % (t % 2), 0, 512 + 2 * i1), R3("ls", c0, c1, s))
+            if t < NV - 1:
+                ACT(R("sw%d" % ((t + 1) % 2), 2 * i0 + s, 2 * i1, 2), src, F.Copy)
+            else:
+                ACT(R("op", 2 * i0 + s, 2 * i1, 2), src, bias=2048.0)
         if t == NV - 1:
-            S(32 * (b - a), ["sw"], ["op" + k], lambda e: e.activation(
-                T.op[:, 32 * a:32 * b], T.sw[:, 32 * a:32 * b], F.Identity, bias=2048.0))
-            D(16384 * (b - a), ["op" + k], [], T.yp[:, 32 * a:32 * b], T.op[:, 32 * a:32 * b])
+            turned("op", "yp", i0, i1, 2, 4, True)
+
+    def write_records(t, h):
+        i0, i1, n, c0, c1 = sizes(h)
+        y, lk, hf, av = "x%d" % ((t + 1) % 2), R("lk", c0, c1), R("hf", i0, i1), R("av", i0, i1)
+        tag[0] = "%d r%d" % (t, h)
+        EITHER("hf%d" % h, hf, ind(R("db%d" % h, 0, 16 * n), lk), bias=-0.25, scale=0.5)
+        TT(av, ind(R("fb%d" % h, 0, 16 * n), lk), hf, A.add)
+        CP(ind(R(y, 16 + 8 * i0, 16 + 8 * i1), R("lx", c0, c1)), av)
+        if t == NV - 1:
+            DMA(R("yx", 8 * i0, 8 * i1), R(y, 16 + 8 * i0, 16 + 8 * i1), 2)
+        elif i0 == 0:
+            ACT(R(y, 2064, 2096), R(y, 16, 48), F.Copy)
 
     def ending(t, h):
-        w, wr = T.w16[:, 256 * t + CW * h:256 * t + CW * h + CW], "w%d%d" % (t, h)
-        p0, p1, p2, p3 = [B("ps%d" % h, b) for b in range(4)]
-        b0, b1, b2, b3 = ["p%d%d" % (h, b) for b in range(4)]
-        hs = str(h)
-        gg, lk, g7, lg, wn = B("gg", h), B("lk", h), B("g7", h), B("lg", h), T.wn
-        gd = T.gd[:, NC * h:NC * h + NC]
-        y, yr = xw[(t + 1) % 2], xn[(t + 1) % 2]
-        pick(h, True)
-        V(NC, ["rs" + hs, "th" + hs], ["gd" + hs], lambda e: e.tensor_tensor(
-            gd, B("rs", h)[:, 15:CW:16], B("th", h)[:, 0:NC], A.is_lt))
+        i0, i1, n, c0, c1 = sizes(h)
+        sw, O = "sw%d" % (t % 2), at(h, "O")
+        gd, bj, rest, new = R("gd", c0, c1), R("bj", i0, i1), R("wz", i0, i1), R(sw, 512 + 2 * i0, 512 + 2 * i1, 2)
+        tag[0] = "%d e%d" % (t, h)
+        pick(h, 1)
+        TT(gd, R("rs", i0 + 15, i1, 16), R("th", c0, c1), A.is_lt)
         if h == NH - 1 and t < NV - 1:
-            ac = T.acol
-            P(b2, ["oneb", "gdc"] + ["gd%d" % k for k in range(NH)],
-              [(p2[:, CW:CW + 17], T.oneb[:], T.gd[:, 0:17], True, True, 17)])
-            V(17, [], ["an"], lambda e: e.tensor_reduce(ac[:, 4:5], p2[:, CW:CW + 17], X.X, A.add, negate=True), b2)
-            V(1, ["an"], ["aq"], lambda e: e.tensor_scalar(ac[:, 8:9], ac[:, 4:5], M5, -M5, A.add, A.add))
-            V(1, ["an", "aq"], ["acol"], lambda e: e.tensor_scalar(
-                ac[:, 0:1], ac[:, 4:5], ac[:, 8:9], 15.5, A.subtract, A.add))
-        SG(CW, DB(h) + ["lk" + hs], ["hf" + hs], lambda e: e.activation(
-            B("hf", h)[:], B("db", h)[:].indirect(lk[:, 0:NC]), F.Identity, bias=-0.25, scale=0.5))
-        VG(CW, FB(h) + ["lk" + hs, "hf" + hs], ["av" + hs], lambda e: e.tensor_tensor(
-            B("av", h)[:], B("fb", h)[:].indirect(lk[:, 0:NC]), B("hf", h)[:], A.add))
-        VG(CW, ["av" + hs, "lx"], [yr + hs], lambda e: e.tensor_copy(
-            y[:, 8 * CW * h:8 * CW * (h + 1)].indirect(T.lx[:, NC * h:NC * h + NC]), B("av", h)[:]), "s")
-        if t == NV - 1:
-            D(2048 * CW, [yr + hs], [], T.yx[:, 8 * CW * h:8 * CW * (h + 1)], y[:, 8 * CW * h:8 * CW * (h + 1)])
-        elif h == 0:
-            S(32, [yr + hs], [yr + "e"], lambda e: e.activation(y[:, 2048:2080], y[:, 0:32], F.Copy))
-        S(CW, [], ["ga" + hs], lambda e: e.activation(gg[:, 0:CW], p3[:, 0:CW], F.Sign, bias=-4096.0), b3)
-        P(b0, ["ga" + hs, "id", "tp", "coh2"],
-          [(p0[:, 0:CW], mat("id"), T.coh[:, 2 * CW:3 * CW], True, False, CW),
-           (p0[:, 0:CW], mat("tp"), gg[:, 0:CW], False, True, CW)])
-        V(CW, ["b32" + hs], ["bj" + hs], lambda e: e.tensor_tensor(B("bj", h)[:], p0[:, 0:CW], B("b32", h)[:], A.mult), b0)
-        P(b1, [wr, "ni", "id"],
-          [(p1[:, CW:2 * CW], mat("id"), w, True, True, CW), (p1[:, 0:CW], mat("ni"), w, True, False, CW)])
-        P(b1, ["bj" + hs, "oh"], [(p1[:, 0:CW], mat("oh"), B("bj", h)[:], False, True, CW)])
-        V(CW, ["ohp" + hs], ["tm" + hs], lambda e: e.tensor_tensor(B("tm", h)[:], p1[:, 0:CW], B("ohp", h)[:], A.mult), b1)
-        V(CW, ["tm" + hs], ["wna" + hs], lambda e: e.tensor_tensor(
-            wn[:, CW * h:CW * h + CW], p1[:, CW:2 * CW], B("tm", h)[:], A.add), b1)
-        V(NC, ["gd" + hs, "t256"], ["g7" + hs], lambda e: e.tensor_tensor(
-            g7[:, 0:NC], T.t256[:, NC * h:NC * h + NC], gd, A.subtract))
-        V(NC, ["g7" + hs], ["lg" + hs], lambda e: e.tensor_scalar(lg[:, 0:NC], g7[:, 0:NC], 256.0, None, A.mult))
+            cnt = R("ps%d" % COUNT, 0, 17)
+            MM([(cnt, one, R("gd", 0, 17), True, True)])
+            op("v", (64, "g", 0), [cnt], [an], lambda e: e.tensor_reduce(an[0], cnt[0], X.X, A.add, negate=True))
+            TS(aq, an, M5, A.add, -M5 - 32, A.add)
+        TS(at(h, "K"), at(h, "S"), col(8), A.is_equal)
+        TT(bj, at(h, "K"), R("bz", 2 * i0 + 1, 2 * i1, 2), A.mult)
+        MM([(R(O[1], O[2] + m, O[3], 16), R("rm", 128 * m, 128 * m + 128), gd, False, False) for m in range(16)])
+        MM([(O, mat("o"), bj, False, True)])
+        TT(R("g7", c0, c1), R("t2", c0, c1), gd, A.subtract)
+        CP(R("lg", c0, c1), R("g7", c0, c1))
+        EITHER("wz%d" % h, rest, ind(R(sw, 512 + 2 * i0, 512 + 2 * i1), R("lg", c0, c1)),
+               bias=2048.0 if t == NV - 1 else 0.0)
         arr = "arr%d%d" % (t, h)
         if t < NV - 1:
-            c0 = 256 * t + CW * h
-            wo = T.wo[:, c0:c0 + CW]
-            VG(CW, WN + ["lg" + hs], ["wo%d%d" % (t, h)], lambda e: e.tensor_copy(wo, wn[:].indirect(lg[:, 0:NC])))
+            src, land = R("wo", 256 * t + i0, 256 * t + i1), R("w16", 256 * (t + 1) + i0, 256 * (t + 1) + i1)
+            TT(src, O, rest, A.max)
+            TT(new, O, rest, A.max)
             if rel is None:
-                to, land, rs, eng = nxt, T.w16[:, 256 + c0:256 + c0 + CW], arr, topo.engines(core, nxt)
+                to, there, rs, eng = nxt, land, arr, topo.engines(core, nxt)
             else:
-                to, land, rs, eng = rel, wo, "hop%d%d" % (t, h), eng_far
-            rid, pid = topo.addr(to, core)
-            op("r", 300, ["wo%d%d" % (t, h)], ["sent%d%d" % (t, h)], lambda e: e.remote_dma(
-                land, wo, T.sem[rs], T.sem.sent, pid, rid, mask_of(eng)), None, len(eng))
-            op("n", PAR["far"], ["sent%d%d" % (t, h)], ["w%d%d" % (t + 1, h)], None, None, (arr, len(eng_far)))
+                to, there, rs, eng = rel, src, "hop%d%d" % (t, h), topo.engines(core, rel)
         else:
-            VG(CW, WN + ["lg" + hs], ["wf" + hs], lambda e: e.tensor_scalar(
-                B("wf", h)[:], wn[:].indirect(lg[:, 0:NC]), 2048.0, None, A.add))
-            rid, pid = topo.addr(home, core)
-            op("r", 300, ["wf" + hs], ["sent%d%d" % (t, h)], lambda e: e.remote_dma(
-                B("lf", h)[:], B("wf", h)[:], T.sem[arr], T.sem.sent, pid, rid, mask_of(eng_far)), None, len(eng_far))
-            op("n", 0.6 * PAR["far"], ["sent%d%d" % (t, h)], ["lf" + hs], None, None, (arr, len(eng_far)))
-            D(512 * CW, ["lf" + hs], [], T.yw[:, CW * h:CW * h + CW], B("lf", h)[:])
-            cur[0] = (t, "z0")
-            write_stock(t, [h])
+            src, land = R("wf", i0, i1), R("lf", i0, i1)
+            TT(src, O, rest, A.max)
+            ACT(new, src, bias=-2048.0)
+            to, there, rs, eng = home, land, arr, eng_far
+        rid, pid = topo.addr(to, core)
+        gone = (None, "gone%d%d" % (t, h), 0, 1, 1, None)
+        op("r", (200, "g", 0), [src], [gone],
+           lambda e: e.remote_dma(there[0], src[0], T.sem[rs], T.sem.sent, pid, rid, mask_of(eng)), len(eng))
+        way = PAR["far"] * (1 if t < NV - 1 else 0.55) + (PAR["first"] if t == 0 and h == 0 else 0)
+        op("n", (way, "g", 0), [gone], [land], None, (arr, len(eng_far)))
+        if t == NV - 1:
+            turned("lf", "yw", i0, i1, 1, 4, True)
+            write_stock(t, i0, i1)
 
     for t in range(NV):
         for h in range(NH):
             stage1(t, h)
-            if h == 0:
-                D(524288, ["offa0"] + xres(t % 2)[:NH], xres((t + 1) % 2)[:NH], xw[(t + 1) % 2][:, 0:2048],
-                  T.xt[:] if t == 0 else xw[t % 2][:, 0:2048])
+        tag[0] = "%d copy" % t
+        DMA(R("x%d" % ((t + 1) % 2), 16, 2064), R("x%d" % (t % 2), 16, 2064) if t else R("xt", 0, 2048), 2,
+            R("off%d" % (NH - 1), 0, 2))
         for h in range(NH):
-            cur[0] = (t, "m%d" % h)
             middle(t, h)
-        write_lists()
+        write_lists(t)
         for h in range(NH):
             gathers(t, 1, h)
-            cur[0] = (t, "e%d" % h)
             ending(t, h)
-        if t < NV - 1:
-            cur[0] = (t, "z0")
-            write_stock(t, list(range(NH)))
+            write_records(t, h)
+        for a, b in STOCK if t < NV - 1 else []:
+            write_stock(t, a, b)
     return ops
 
 
 QUEUE = {"v": "v", "s": "s", "p": "p", "g": "g", "r": "g", "y": "y", "n": "n"}
 
 
-def plan(ops):
+def needs(ops):
     n = len(ops)
-    deps = [set() for _ in range(n)]
-    soft = [set() for _ in range(n)]
-    wr, rd, bk = {}, {}, {}
-    for i, (e, c, r, w, bank, fn, sem, key) in enumerate(ops):
-        for k in r:
-            if k in wr:
-                deps[i].add(wr[k])
-        for k in w:
-            if k in wr:
-                deps[i].add(wr[k])
-            deps[i].update(rd.get(k, []))
-        for k in r:
-            rd.setdefault(k, []).append(i)
-        for k in w:
-            wr[k] = i
-            rd[k] = []
-        if bank:
+    deps, soft = [set() for _ in range(n)], [set() for _ in range(n)]
+    seen, bk = {}, {}
+    for i, o in enumerate(ops):
+        banks = set()
+        for acc, write in ((o[2], False), (o[3], True)):
+            for name, a, b in acc:
+                if name in SCRATCH and SCRATCH[name][0] == "psum":
+                    banks.add(name)
+                for a2, b2, j, w2 in seen.get(name, []):
+                    if a < b2 and a2 < b and (write or w2) and not o[0] == ops[j][0] == "p":
+                        deps[i].add(j)
+        for name, a, b in o[3]:
+            seen[name] = [z for z in seen.get(name, []) if not (a <= z[0] and z[1] <= b)] + [(a, b, i, True)]
+        for name, a, b in o[2]:
+            seen.setdefault(name, []).append((a, b, i, False))
+        for bank in banks:
             run, before = bk.get(bank, ([], []))
-            if run and ops[run[0]][0] == e:
+            if run and ops[run[0]][0] == o[0]:
                 soft[i].add(run[-1])
                 deps[i].update(before)
                 run.append(i)
@@ -517,43 +556,153 @@ def plan(ops):
                 deps[i].update(run)
                 bk[bank] = ([i], run)
         deps[i].discard(i)
-    users = [[] for _ in range(n)]
-    for i in range(n):
-        for j in deps[i] | soft[i]:
-            users[j].append(i)
-    lat = PAR["lat"]
-    chain = [0.0] * n
-    for i in range(n - 1, -1, -1):
-        chain[i] = ops[i][1] + lat + max([chain[j] for j in users[i]] + [0.0])
-    rank = [1e9 if o[7] is None else 10 * o[7][0] + KEYS[o[7][1]] + sum(o[7][2:]) for o in ops]
-    for i in range(n - 1, -1, -1):
-        rank[i] = min([rank[i]] + [rank[j] for j in users[i]])
-    prio = [(-rank[i], chain[i] * (1.0 + JIT[1] * (((i + 1) * JIT[0] * 0.6180339887) % 1.0))) for i in range(n)]
-    hold = lambda i: 60.0 if ops[i][0] == "y" else 0.0 if ops[i][0] == "n" else ops[i][1]
-    free = {q: 0.0 for q in QUEUE.values()}
-    left = [len(deps[i] | soft[i]) for i in range(n)]
-    ready_at = [0.0] * n
-    ready = [i for i in range(n) if left[i] == 0]
-    order, end, start = [], [0.0] * n, [0.0] * n
-    while ready:
-        t0, q0 = min((max(ready_at[i], free[QUEUE[ops[i][0]]]), QUEUE[ops[i][0]]) for i in ready)
-        cand = [i for i in ready if QUEUE[ops[i][0]] == q0]
-        i = max([i for i in cand if ready_at[i] <= t0], key=lambda j: (prio[j], -j))
-        soon = [j for j in cand
-                if ready_at[j] > t0 and prio[j] > prio[i] and ready_at[j] - t0 < min(SOON[0], SOON[1] * hold(i))]
-        if soon:
-            i = max(soon, key=lambda j: (prio[j], -j))
-        ready.remove(i)
-        start[i] = max(t0, ready_at[i])
-        end[i] = start[i] + ops[i][1]
-        free[q0] = start[i] + hold(i)
-        order.append(i)
-        for j in users[i]:
-            ready_at[j] = max(ready_at[j], end[i] + lat if i in deps[j] else start[i])
+    return deps, soft
+
+
+def turned_round(fore):
+    back = [[] for _ in fore]
+    for i, before in enumerate(fore):
+        for j, gap in before:
+            back[j].append((i, gap))
+    return back
+
+
+def first_order(ops, cost, hold, fore):
+    n = len(ops)
+    fore = [list(x) for x in fore]
+    steps = {}
+    for i, o in enumerate(ops):
+        if o[6][2:3] == "g" and o[0] in LONG:
+            steps.setdefault((o[6][0], o[0], o[3][0][0][0] + o[6][3:]), []).append(i)
+    for q in LONG:
+        row = [steps[str(t), q, name].pop(0) for t in range(NV) for name in LONG[q].split()]
+        for j, i in zip(row, row[1:]):
+            fore[i].append((j, 0.0))
+    back = turned_round(fore)
+    left = [len(x) for x in fore]
+    seq = [i for i in range(n) if not left[i]]
+    for i in seq:
+        for j, gap in back[i]:
             left[j] -= 1
-            if left[j] == 0:
-                ready.append(j)
-    return order, deps, start, end, soft
+            if not left[j]:
+                seq.append(j)
+    chain = [0.0] * n
+    for i in reversed(seq):
+        chain[i] = cost[i] + max([chain[j] + gap for j, gap in back[i]] + [0.0])
+    left = [len(x) for x in fore]
+    free = {q: 0.0 for q in QUEUE.values()}
+    ready = {q: [i for i in range(n) if not left[i] and QUEUE[ops[i][0]] == q] for q in free}
+    at, start = [0.0] * n, [0.0] * n
+    for _ in range(n):
+        t0, q = min((max(min(at[i] for i in row), free[q]), q) for q, row in ready.items() if row)
+        i = min((j for j in ready[q] if at[j] <= t0), key=lambda j: (-chain[j], j))
+        soon = [j for j in ready[q] if t0 < at[j] < t0 + min(300.0, 0.35 * hold[i]) and chain[j] > chain[i]]
+        if soon:
+            i = min(soon, key=lambda j: (-chain[j], j))
+        ready[q].remove(i)
+        start[i] = max(t0, at[i])
+        free[q] = start[i] + hold[i]
+        for j, gap in back[i]:
+            at[j] = max(at[j], start[i] + cost[i] + gap)
+            left[j] -= 1
+            if not left[j]:
+                ready[QUEUE[ops[j][0]]].append(j)
+    return sorted(range(n), key=lambda i: (start[i], i))
+
+
+def survey(order, queue, cost, hold, fore, back):
+    n, nq = len(order), max(queue) + 1
+    end, why, before = [0.0] * n, [None] * n, []
+    free, last = [0.0] * nq, [None] * nq
+    for i in order:
+        before.append(tuple(free))
+        q = queue[i]
+        t, w = free[q], (last[q], True)
+        for j, gap in fore[i]:
+            if end[j] + gap >= t:
+                t, w = end[j] + gap, (j, False)
+        end[i], free[q], last[q], why[i] = t + cost[i], t + hold[i], i, w
+    top = max(end)
+    i, pairs = end.index(top), []
+    while why[i][0] is not None:
+        if why[i][1]:
+            pairs.append((why[i][0], i))
+        i = why[i][0]
+    rest, after, ahead = [0.0] * n, [None] * n, [0.0] * nq
+    for k in range(n - 1, -1, -1):
+        after[k] = tuple(ahead)
+        i = order[k]
+        t = max(cost[i], hold[i] + ahead[queue[i]])
+        for j, gap in back[i]:
+            if cost[i] + gap + rest[j] > t:
+                t = cost[i] + gap + rest[j]
+        rest[i] = ahead[queue[i]] = t
+    return top, end, before, pairs, rest, after
+
+
+def plan(ops):
+    n = len(ops)
+    deps, soft = needs(ops)
+    queue = ["vspgyn".index(QUEUE[o[0]]) for o in ops]
+    cost = [(o[1][0] + PAR[o[1][1]] * o[1][2]) * (PAR["slow"] if o[0] in "vspg" else 1) for o in ops]
+    hold = [max(60.0, c - PAR["dma"]) if o[0] == "y" else 0.0 if o[0] == "n" else c for o, c in zip(ops, cost)]
+    fore, reach = [], []
+    for i in range(n):
+        near, seen = [], 0
+        for j in sorted(deps[i] | soft[i], reverse=True):
+            if not seen >> j & 1:
+                near.append((j, PAR["lat"] if j in deps[i] else 0.0))
+            seen |= reach[j] | 1 << j
+        fore.append(near)
+        reach.append(seen)
+    back = turned_round(fore)
+    state = [PAR["seed"]]
+
+    def draw(k):
+        state[0] = (state[0] * 1103515245 + 12345) % 2 ** 31
+        return (state[0] >> 8) % k
+
+    def settle(order):
+        end = survey(order, queue, cost, hold, fore, back)[1]
+        order = sorted(order, key=lambda i: end[i] - cost[i])
+        pos = [0] * n
+        for k, i in enumerate(order):
+            pos[i] = k
+        return (order, pos) + survey(order, queue, cost, hold, fore, back)
+
+    order, pos, top, end, before, pairs, rest, after = settle(first_order(ops, cost, hold, fore))
+    best = (top, order)
+    for it in range(PAR["tries"]):
+        j, i = pairs[draw(len(pairs))]
+        ahead = draw(2) == 1
+        lo, hi = pos[j], pos[i]
+        for _ in range(draw(4) - 1):
+            k = lo - 1 if ahead else hi + 1
+            while 0 <= k < n and queue[order[k]] != queue[i]:
+                k += -1 if ahead else 1
+            if 0 <= k < n:
+                lo, hi = (k, hi) if ahead else (lo, k)
+        move, todo = set(), [order[hi] if ahead else order[lo]]
+        while todo:
+            x = todo.pop()
+            if x not in move and lo <= pos[x] <= hi:
+                move.add(x)
+                todo.extend(y for y, gap in (fore if ahead else back)[x])
+        if order[lo if ahead else hi] in move:
+            continue
+        part = order[lo:hi + 1]
+        part = [x for x in part if (x in move) == ahead] + [x for x in part if (x in move) != ahead]
+        free, new, guess = list(before[lo]), {}, 0.0
+        for x in part:
+            t = max([free[queue[x]]] + [new.get(y, end[y]) + gap for y, gap in fore[x]])
+            new[x], free[queue[x]] = t + cost[x], t + hold[x]
+            guess = max([guess] + [new[x] + gap + rest[y] for y, gap in back[x] if pos[y] > hi])
+        guess = max([guess] + [a + b for a, b in zip(free, after[hi])])
+        if guess <= top + PAR["warm"] * 0.1 ** (it / PAR["tries"]) * -math.log((draw(1000) + 1) / 1001.0):
+            order, pos, top, end, before, pairs, rest, after = settle(order[:lo] + part + order[hi + 1:])
+            if top < best[0]:
+                best = (top, order)
+    return best[1], deps, best[0]
 
 
 def rank_program(g, core, T, topo):
@@ -562,24 +711,19 @@ def rank_program(g, core, T, topo):
         for r in range(N):
             src, dst = T.cores[r], T.cores[(r + 1) % N]
             if relay_of(src, dst, topo) == core:
-                relay_program(g, core, T, topo, dst)
+                relay_program(g, core, T, topo, src, dst)
         return
-    ops = build(g, core, T, topo)
+    ops = build(core, T, topo)
     if "order" not in PLAN:
         PLAN["order"] = plan(ops)
     order, deps = PLAN["order"][0:2]
-    if ORDER:
-        order = [int(x) for x in ORDER.split(",")]
-        assert sorted(order) == list(range(len(ops)))
-        at = {i: k for k, i in enumerate(order)}
-        assert all(at[j] < at[i] for i in order for j in deps[i] | PLAN["order"][4][i])
     eng = {"v": g.vector, "s": g.scalar, "p": g.tensor, "g": g, "r": g, "y": g.sync}
     count = {"v": 0, "s": 0, "p": 0, "g": 0}
     done = {}
     seen = {q: {} for q in "vspgy"}
     sent = 0
     for i in order:
-        e, c, r, w, bank, fn, sem, key = ops[i]
+        e, c, r, w, fn, sem, name = ops[i]
         if e == "n":
             done[i] = sem
             continue

import math
from concourse.mybir import AluOpType as A, ActivationFunctionType as F, AxisListType as X

NV = 3
PARTS = [(0, 96), (96, 160), (160, 256)]
NH = len(PARTS)
PIECES = {(0, 0): "32A+ 32a+ 32a", (0, 1): "32a+ 32a", (0, 2): "32a+ 32a+ 32a",
          (1, 0): "32a+ 32a+ 32a", (1, 1): "32a+ 32a", (1, 2): "32a+ 48a 16a"}
BANKS = [(0, 1, 1, 1), (2, 3, 3, 3), (4, 5, 5, 5)]
SPLIT = [(0, 0), (1, 0), (0, 2), (1, 2)]
ON_VECTOR = "bz0 bz1 bz2"
STOCK = [(0, 256)]
COUNT = 7
K = 8192.0
M5 = 1.5 * 2.0 ** 28

f32, bf, f16, i32, u16 = "float32", "bfloat16", "float16", "int32", "uint16"
MATS = ["id", "up", "o", "ni", "ihi", "ilo", "uphi", "uplo", "um", "tm", "tp2", "tpk", "tq", "sk",
        "ohi", "olo"]
BANDS = {"en": 0, "ep": 160, "ew": 320, "dd": 480, "d0": 640, "d15": 768}
SCRATCH = {
    "wi": ("sbuf", [128, 256], i32), "pi": ("sbuf", [128, 512], i32), "wti": ("sbuf", [128, 4], i32),
    "x0": ("sbuf", [128, 2096], bf), "x1": ("sbuf", [128, 2096], bf),
    "sw0": ("sbuf", [128, 1024], f32), "sw1": ("sbuf", [128, 1024], f32),
    "op": ("sbuf", [128, 512], f32),
    "mats": ("sbuf", [128, 128 * len(MATS)], bf), "imd": ("sbuf", [128, 128], f32),
    "rm": ("sbuf", [128, 16 * 128], bf), "bands": ("sbuf", [128, 896], bf),
    "one": ("sbuf", [128, 128], bf), "c8k": ("sbuf", [128, 128], bf), "cs": ("sbuf", [128, 256], bf),
    "bz": ("sbuf", [128, 512], f32), "cm": ("sbuf", [128, 256], bf), "coh": ("sbuf", [128, 256], bf),
    "ck": ("sbuf", [128, 256], f16), "msk": ("sbuf", [128, 128], bf),
    "ia": ("sbuf", [128, 16], i32), "ic": ("sbuf", [128, 128], i32), "ie": ("sbuf", [128, 32], i32),
    "cols": ("sbuf", [128, 32], f32), "tl": ("sbuf", [128, 16], f32), "b16": ("sbuf", [128, 16], f32),
    "ct": ("sbuf", [128, 16], f32), "cb": ("sbuf", [128, 16], f32), "t2": ("sbuf", [128, 16], f32),
    "sc": ("sbuf", [128, 2, 16], f32), "sx": ("sbuf", [128, 2, 16], f32), "hh": ("sbuf", [128, 2, 16], f32),
    "ls": ("sbuf", [128, 2, 16], u16), "gd": ("sbuf", [128, 32], bf), "acol": ("sbuf", [128, 16], f32),
    "ui": ("sbuf", [128, 16], i32), "sm": ("sbuf", [128, 32], i32), "sm2": ("sbuf", [128, 16], f32),
    "lx": ("sbuf", [128, 16], u16), "ix": ("sbuf", [128, 16], i32), "lk": ("sbuf", [128, 16], u16),
    "kb": ("sbuf", [128, 16], bf), "th": ("sbuf", [128, 16], f32), "u9": ("sbuf", [128, 16], i32),
    "lb": ("sbuf", [128, 16], u16), "g7": ("sbuf", [128, 16], f32), "lg": ("sbuf", [128, 16], u16),
    "w16": ("sbuf", [128, NV * 256], f16),
    "wo": ("sbuf", [128, (NV - 1) * 256], f16),
    "wf": ("sbuf", [128, 256], f32), "lf": ("sbuf", [128, 256], f32),
}
for _n, _d in (("rs", i32), ("ga", bf), ("gb", bf), ("fk", bf), ("r1", f32), ("wz", f32), ("bj", f16), ("hf", f32),
               ("av", i32)):
    SCRATCH[_n] = ("sbuf", [128, 256], _d)
for _h, (_a, _b) in enumerate(PARTS):
    _n = _b - _a
    for _s, _w, _d in (("off", 2 * _n, u16), ("xi", 2 * _n, i32), ("xj", 4 * _n, i32), ("p32", _n, f32),
                       ("tt", 2 * _n, f16),
                       ("fb", 16 * _n, bf), ("db", 16 * _n, bf)):
        SCRATCH["%s%d" % (_s, _h)] = ("sbuf", [128, _w], _d)
    SCRATCH["ab%d" % _h] = ("sbuf", [128, _n // 16, 16, 16], bf)
for _b in range(8):
    SCRATCH["ps%d" % _b] = ("psum", [128, 512], f32)

SEMAPHORES = (["cv", "cs", "cp", "cg", "sent"] + ["d%d" % k for k in range(30)]
              + ["arr%d%d" % (t, h) for t in range(NV) for h in range(NH)]
              + ["hop%d%d" % (t, h) for t in range(NV - 1) for h in range(NH)])

PAR = {"g": 1.56, "s": 3.5, "pe": 0.56, "lat": 250.0, "far": 5000.0, "first": 3000.0, "dma": 1800.0, "bw": 200.0,
       "slow": 1.15, "run": 4, "tries": 50000, "warm": 200.0, "seed": 1}
LONG = {"s": "f00 f00 a00 a00 a00 f01 f01 f02 f02 f02 a01 a01 a02 a02 a02 f10 f10 a10 f10 a10 a10 f11 f11 f12 a11 "
             "f12 f12 a11 a12 a12 a12",
        "v": "f00 d00 d00 d00 d01 d01 d02 d02 d02 d10 d10 d10 d11 d12 d11 d12 d12"}
PLAN = {}


def relay_of(src, dst, topo):
    if topo.may_write(src, dst):
        return None
    can = [c for c in topo.cores_of(src) if topo.may_write(c, dst)]
    near = [c for c in can if topo.die(c) == topo.die(src)]
    return (near or can)[0]


def mask_of(engines):
    m = 0
    for e in engines:
        m |= 1 << e
    return m


def relay_program(g, core, T, topo, src, dst):
    eng = topo.engines(core, dst)
    rid, pid = topo.addr(dst, core)
    n = 0
    for t in range(NV - 1):
        for h, (a, b) in enumerate(PARTS):
            g.wait_ge(T.sem["hop%d%d" % (t, h)], len(topo.engines(src, core)))
            g.remote_dma(T.w16[:, 256 * (t + 1) + a:256 * (t + 1) + b], T.wo[:, 256 * t + a:256 * t + b],
                         T.sem["arr%d%d" % (t, h)], T.sem.sent, pid, rid, mask_of(eng))
            n += len(eng)
    g.wait_ge(T.sem.sent, n)


def build(core, T, topo):
    ops = []
    N = len(T.cores)
    rank = T.rank_of(core)
    nxt = T.cores[(rank + 1) % N]
    home = T.cores[(rank - (NV - 1)) % N]
    rel = relay_of(core, nxt, topo)
    eng_far = topo.engines(core, home)
    tag = ["c"]

    def R(name, a, b, step=1):
        return (T[name][:, a:b:step] if step > 1 else T[name][:, a:b], name, a, b, len(range(a, b, step)), None)

    def R4(name, c0, c1, m=None, place=None):
        t = T[name]
        ap = t[:, c0:c1] if m is None and place is None else t[:, c0:c1, m, :] if place is None else t[:, c0:c1, :, place]
        return (ap, name, 256 * c0, 256 * c1, (c1 - c0) * (256 if m is None and place is None else 16), None)

    def R3(name, c0, c1, s=None):
        if s is None:
            return (T[name][:, :, c0:c1], name, 0, 32, 2 * (c1 - c0), None)
        return (T[name][:, s, c0:c1], name, 0, 32, c1 - c0, None)

    def ind(win, off):
        return (win[0].indirect(off[0]), win[1], win[2], win[3], 16 * off[4], off)

    def mat(name):
        k = 128 * MATS.index(name)
        return R("mats", k, k + 128)

    def band(name, m):
        return R("bands", BANDS[name] + 16 - m, BANDS[name] + 144 - m)

    def col(k):
        return R("cols", k, k + 1)

    def ap(x):
        return x[0] if isinstance(x, tuple) else x

    def op(q, cost, reads, writes, fn, sem=None):
        r = [x for x in reads if isinstance(x, tuple)]
        r += [x[5] for x in r + writes if x[5]]
        ops.append((q, cost, [x[1:4] for x in r], [x[1:4] for x in writes], fn, sem, tag[0]))

    def short(*xs):
        return all(SCRATCH[x[1]][2] in (bf, f16, u16) for x in xs)

    def price(q, out, a, n):
        if out[5]:
            return (60, "s", out[4])
        if a[5]:
            return (60 if q == "v" else 78, "g", a[4])
        return (max(64.0, n), "g", 0)

    def TT(out, a, b, alu):
        two = SCRATCH[a[1]][0] == SCRATCH[b[1]][0]
        op("v", price("v", out, a, a[4] * (2 if two else 1)), [a, b], [out],
           lambda e: e.tensor_tensor(out[0], a[0], b[0], alu))

    def TS(out, a, s1, op0, s2=None, op1=None):
        cost = price("v", out, a, a[4] * (0.5 if short(out, a) else 1))
        if op1 is None:
            op("v", cost, [a, s1], [out], lambda e: e.tensor_scalar(out[0], a[0], ap(s1), None, op0))
        else:
            op("v", cost, [a, s1, s2], [out], lambda e: e.tensor_scalar(out[0], a[0], ap(s1), ap(s2), op0, op1))

    def CP(out, a):
        op("v", price("v", out, a, a[4] * (0.5 if short(out, a) else 1)), [a], [out],
           lambda e: e.tensor_copy(out[0], a[0]))

    def SCAN(out, d0, d1, op0, op1):
        op("v", (max(64, out[4]), "g", 0), [d0, d1], [out],
           lambda e: e.tensor_tensor_scan(out[0], d0[0], d1[0], 0.0, op0, op1))

    def SET(out, v):
        op("v", (max(64.0, out[4] * (0.5 if short(out) else 1)), "g", 0), [], [out], lambda e: e.memset(out[0], v))

    def ACT(out, a, func=F.Identity, bias=0.0, scale=1.0):
        op("s", price("s", out, a, a[4]), [a, bias, scale], [out],
           lambda e: e.activation(out[0], a[0], func, bias=ap(bias), scale=ap(scale)))

    def EITHER(name, out, a, func=F.Identity, bias=0.0, scale=1.0):
        if name not in ON_VECTOR.split():
            ACT(out, a, func, bias, scale)
        elif func == F.Sign:
            TS(out, a, bias[6], A.is_gt, 2.0, A.mult)
        elif func == F.Relu:
            TS(out, a, bias, A.add, 0.0, A.max)
        else:
            TS(out, a, scale, A.mult, bias, A.add)

    def MM(mm):
        if len(mm) > PAR["run"]:
            MM(mm[:PAR["run"]])
            MM(mm[PAR["run"]:])
            return
        cost = sum(max(64, m[2][4]) * (4 if SCRATCH[m[1][1]][2] == f32 else 1) for m in mm)
        op("p", (0, "pe", cost), [m[1] for m in mm] + [m[2] for m in mm], [m[0] for m in mm],
           lambda e: [e.matmul(m[0][0], m[1][0], m[2][0], m[3], m[4]) for m in mm])

    def IOTA(out, pattern, base, cm):
        op("g", (160 + 2 * out[4], "g", 0), [], [out], lambda e: e.iota(out[0], pattern, base, cm))

    def SEL(out, a, pattern, cmp, base, cm):
        op("g", (205 + 2 * out[4], "g", 0), [a], [out],
           lambda e: e.affine_select(out[0], a[0], pattern, cmp, 0.0, base, cm))

    nd = [0]

    def DMA(out, a, size, after=None):
        op("y", (PAR["dma"] + 128 * size * out[4] / PAR["bw"], "g", 0), [a, after], [out],
           lambda e: e.dma_start(out[0], a[0]), "d%d" % nd[0])
        nd[0] += 1

    def turned(buf, hbm, a, b, k, size, store=False):
        here, there = R(buf, k * a, k * b), R(hbm, k * a, k * b)
        DMA(*((there, here) if store else (here, there)), size)

    turned("wi", "wd", *PARTS[0], 1, 4)
    DMA(R("x0", 16, 2064), R("xt", 0, 2048), 2)
    turned("wi", "wd", PARTS[0][1], 256, 1, 4)
    DMA(R("x0", 2064, 2096), R("xt", 0, 32), 2)
    DMA(R("wti", 0, 1), (T.wt[:], "wt", 0, 1, 1, None), 4)
    DMA(R("pi", 0, 512), R("pd", 0, 512), 4, R("wi", 0, 1))

    one, c8k = R("one", 0, 128), R("c8k", 0, 128)
    SET(one, 1.0)
    SEL(mat("id"), one, [[-1, 128]], A.is_equal, 0, 1)
    SEL(mat("up"), one, [[-1, 128]], A.is_equal, -1, 1)
    k0 = 128 * MATS.index("up")
    SEL(R("mats", k0 + 15, k0 + 128, 16), R("one", 0, 8), [[-16, 8]], A.is_equal, 0, 1)
    for k, v in enumerate((2080.0, 3232.0)):
        SET(R("cs", 128 * k, 128 * k + 128), v)
    an, aq = R("acol", 0, 1), R("acol", 1, 2)
    SET(an, 16.0)
    SET(aq, 0.0)
    for x in ("x0", "x1"):
        SET(R(x, 0, 16), 0.0)
    for name, src, k in (("ihi", "id", 3232), ("ilo", "id", 2080), ("uphi", "up", 3232), ("uplo", "up", 2080),
                         ("ni", "id", -1)):
        ACT(mat(name), mat(src), scale=float(k))
    for a, b in PARTS:
        TS(R("w16", a, b), R("wi", a, b), -2048.0, A.add)
    SEL(mat("o"), one, [[-16, 8], [0, 16]], A.is_ge, 0, 1)
    SEL(mat("o"), mat("o"), [[16, 8], [0, 16]], A.is_ge, 15, -1)
    for name, k in (("ohi", 3232), ("olo", 2080)):
        ACT(mat(name), mat("o"), scale=float(k))
    IOTA(R("ia", 0, 16), [[-1, 16]], 128, 1)
    TS(R("ia", 0, 16), R("ia", 0, 16), 15, A.bitwise_and)
    CP(col(0), R("ia", 0, 1))
    ACT(col(1), col(0), scale=16.0)
    CP(col(2), R("wti", 0, 1))
    TS(R("cols", 16, 32), R("ia", 0, 16), 0.0, A.is_equal)
    ACT(col(3), col(16), scale=K, bias=-4096.0)
    TS(col(4), col(17), col(16), A.subtract, 4096.0, A.mult)
    ACT(col(5), col(0), scale=-K, bias=-0.5)
    ACT(col(6), col(0), scale=-K, bias=-4096.0)
    ACT(col(7), col(16), scale=-K)
    ACT(col(8), col(0), scale=K)
    ACT(col(9), col(0), scale=K, bias=0.5)
    ACT(col(10), col(0), scale=K, bias=4096.0)
    SET(R("bands", 0, 896), 0.0)
    k0 = 128 * MATS.index("o")
    o8 = R("mats", k0, k0 + 128, 16)
    for name, at, k in (("en", 16, -2048.0), ("ep", 16, 4096.0), ("ew", 16, col(2)), ("dd", 15, 1.0), ("dd", 17, -1.0),
                        ("d0", 15, 1.0), ("d0", 1, -1.0), ("d15", 14, 1.0), ("d15", 0, -1.0)):
        ACT(R("bands", BANDS[name] + at, BANDS[name] + at + 113, 16), o8, scale=k)

    def dk(k):
        if k in (0, 15):
            return R("bands", BANDS["d%d" % k], BANDS["d%d" % k] + 128)
        return band("dd", k)

    IOTA(R("ic", 0, 128), [[256, 8], [1, 16]], 0, 0)
    SET(R("ck", 0, 128), 0.0)
    TS(R("ck", 128, 256), R("ic", 0, 128), col(1), A.add)
    SET(R("msk", 0, 128), 0.0)
    SET(R("msk", 0, 128, 16), 2.0 ** 25)
    SET(c8k, K)
    for m in range(16):
        SEL(R("rm", 128 * m, 128 * m + 128), c8k, [[-16, 8], [0, 16]], A.is_equal, -m, 1)
    q0, q1, q2, q3 = [R("ps%d" % COUNT, 128 * k, 128 * k + 128) for k in range(4)]
    MM([(q0, mat("id"), mat("up"), True, False), (q0, mat("id"), mat("ni"), False, True),
        (q1, mat("up"), mat("id"), True, False), (q1, mat("id"), mat("ni"), False, True)])
    ACT(mat("tp2"), q1)
    ACT(mat("um"), q0)
    ACT(mat("tm"), q0, scale=-0.5)
    ACT(mat("tpk"), q1, scale=K / 2)
    ACT(R("imd", 0, 128), q1, scale=-1.0)
    MM([(q2, mat("up"), mat("tp2"), True, True),
        (q3, mat("up"), mat("tp2"), True, False), (q3, mat("ni"), mat("tp2"), False, True)])
    ACT(mat("tq"), q2, scale=0.5)
    ACT(mat("sk"), q3, scale=2048.0)
    ACT(R("coh", 0, 128), one, scale=col(31))
    ACT(R("coh", 128, 256), one, scale=col(17))
    ACT(R("cm", 0, 128), c8k, scale=col(16), bias=-2 * K)
    ACT(R("cm", 128, 256), c8k, scale=col(16), bias=2048 - 2 * K)
    for a in (0, 256):
        ACT(R("bz", a, a + 256, 2), one, scale=0.0)
    for a, b in PARTS:
        IOTA(R("ie", a // 16, b // 16), [[16, (b - a) // 16]], 0, 0)
    IOTA(R("ie", 16, 32), [[16, 16]], 0, 0)
    TS(R("tl", 0, 16), R("ie", 0, 16), col(0), A.add)
    TS(R3("sc", 0, 16, 0), R("ie", 16, 32), col(0), A.add, 2.0, A.mult)
    ACT(R3("sc", 0, 16, 1), R3("sc", 0, 16, 0), bias=1.0)
    for s in range(2):
        ACT(R3("sx", 0, 16, s), R("tl", 0, 16), scale=0.0, bias=512.0 - s)
    for name, k, c in (("b16", 16, 0), ("ct", 32, -1000), ("cb", 8, 0), ("t2", 2, 1)):
        ACT(R(name, 0, 16), R("tl", 0, 16), scale=float(k), bias=float(c))
    SET(R("gd", 16, 17), -16.25 / 128)
    for a in (0, 256):
        TS(R("sw0", a, a + 256), R("pi", a, a + 256), -2048.0, A.add)

    def sizes(h):
        i0, i1 = PARTS[h]
        return i0, i1, i1 - i0, i0 // 16, i1 // 16

    def at(h, what, a=0, b=1, step=1):
        n = PARTS[h][1] - PARTS[h][0]
        bank = BANKS[h]["SKDOI".index(what) - 1 if what != "S" else 0]
        base = n if what == "K" else 0
        if what in "OI" and BANKS[h][1] == bank:
            base = n
        return R("ps%d" % bank, base + int(a * n), base + int(b * n), step)

    def lists(h, st):
        i0, i1, n, c0, c1 = sizes(h)
        for a, b in ((0, n), (n, 2 * n)) if (st, h) in SPLIT else ((0, 2 * n),):
            xi = R("xi%d" % h, a, b)
            TS(xi, R("xj%d" % h, 2 * a + 1, 2 * b, 2) if st else xi, 5, A.arith_shift_right, 2047, A.bitwise_and)
            TS(R("off%d" % h, a, b), xi, an, A.add, aq, A.subtract)

    def gathers(t, st, h):
        i0, i1, n, c0, c1 = sizes(h)
        x = R("x%d" % (t % 2), 0, 2096)
        fb, db, ab, off = [s + str(h) for s in ("fb", "db", "ab", "off")]
        tag[0] = "%d g%d%d" % (t, st, h)
        Kb, Db = at(h, "K")[1], at(h, "D")[1]
        MM([(at(h, "K"), mat("id"), R("ck", 128, 128 + n), True, False)])
        once = PIECES[st, h].count("+") == len(PIECES[st, h].split()) - 1
        if st == 0 and not once:
            MM([(at(h, "D"), mat("id"), R("ck", 0, n), True, False)])
        a = first = 0
        for word in PIECES[st, h].split():
            b = a + int(word.rstrip("aA+"))
            f, o1, o2 = R(fb, 16 * a, 16 * b), R(off, a, b), R(off, n + a, n + b)
            if "A" in word:
                CP(f, ind(x, o1))
            else:
                ACT(f, ind(x, o1), F.Copy)
            TT(R(db, 16 * a, 16 * b), ind(x, o2), f, A.subtract)
            ACT(R4(ab, a // 16, b // 16), R(db, 16 * a, 16 * b), F.Abs)
            a = b
            if word.endswith("+"):
                continue
            MM([(R(Kb, n + first, n + b), band("ep" if st else "en", m), R4(ab, first // 16, b // 16, m=m), False,
                 b == n and m == 15) for m in range(16)])
            if st == 0:
                MM([(R(Db, first, b), dk(m), R4(ab, first // 16, b // 16, place=m), once and m == 0, False)
                    for m in range(16)])
            first = b
        assert a == n

    def pick(h, st):
        i0, i1, n, c0, c1 = sizes(h)
        SCAN(R("rs", i0, i1), R("msk", 0, n), at(h, "K"), A.add, A.min)
        TS(R("ix", c0, c1), R("rs", i0 + 15, i1, 16), 2047, A.bitwise_and)
        TT(R("kb", c0, c1), R("ix", c0, c1), R("b16", c0, c1), A.subtract)
        CP(R("lk", c0, c1), R("ix", c0, c1))
        if st:
            MM([(at(h, "S"), mat("id"), R("ck", 0, n), True, False)])
        MM([(R(at(h, "S" if st else "D")[1], m, n, 16), R("rm", 128 * m, 128 * m + 128), R("kb", c0, c1), False,
             m == 15) for m in range(16)])

    def stage1(t, h):
        i0, i1, n, c0, c1 = sizes(h)
        w, p32 = R("w16", 256 * t + i0, 256 * t + i1), R("p32%d" % h, 0, n)
        Ia, Ib, Ic = [at(h, "I", k, k + 1) for k in range(3)]
        tag[0] = "%d a%d" % (t, h)
        MM([(Ia, mat("up"), w, True, True), (Ib, mat("ihi"), w, True, False), (Ib, mat("uplo"), w, False, True)])
        MM([(Ic, mat("ilo"), w, True, False), (Ic, mat("uphi"), w, False, True)])
        TT(p32, Ia, w, A.mult)
        TT(R("xi%d" % h, 0, n), Ib, p32, A.add)
        TT(R("xi%d" % h, n, 2 * n), Ic, p32, A.add)
        lists(h, 0)
        gathers(t, 0, h)

    def middle(t, h):
        i0, i1, n, c0, c1 = sizes(h)
        w, sw, tt = R("w16", 256 * t + i0, 256 * t + i1), "sw%d" % (t % 2), "tt%d" % h
        ga, gb, r1 = [R(s, i0, i1) for s in ("ga", "gb", "r1")]
        Oa, Ob, Oc, Od = [at(h, "O", k, k + 1) for k in range(4)]
        I, e0 = at(h, "I")[1:3]
        even = R(I, e0, e0 + 4 * n, 2)
        u = R(at(h, "S")[1], 0, c1 - c0)
        tag[0] = "%d m%d" % (t, h)
        o_start = [(at(h, "O", 0, 2), mat("id"), R("coh", 128 - n, 128 + n), True, False)]
        i_start = [(even, mat("id"), R("cs", 128 - n, 128 + n), True, False)]
        if BANKS[h][2] != BANKS[h][1]:
            MM(o_start)
            o_start = []
        if BANKS[h][3] not in BANKS[h][1:3]:
            MM(i_start)
            i_start = []
        pick(h, 0)
        EITHER("fk%d" % h, R("fk", i0, i1), ind(R("fb%d" % h, 0, 16 * n), R("lk", c0, c1)))
        MM([(u, band("ew", m), R("fk", i0 + m, i1, 16), m == 0, m == 15) for m in range(16)])
        CP(R("ui", c0, c1), u)
        EITHER("ga%d" % h, ga, at(h, "D"), F.Sign, bias=col(5) + (col(9),))
        TS(R("u9", c0, c1), R("ui", c0, c1), 511, A.bitwise_and)
        CP(R("lb", c0, c1), R("u9", c0, c1))
        EITHER("bz%d" % h, R("bz", 2 * i0 + 1, 2 * i1, 2), ind(R(sw, 0, 512), R("lb", c0, c1)))
        TT(R("th", c0, c1), R("ct", c0, c1), R("rs", i0 + 15, i1, 16), A.subtract)
        MM(o_start + [(Oa, mat("tm"), ga, False, False), (Ob, mat("tq"), ga, False, True)])
        TT(R(tt, 0, n), Oa, w, A.mult)
        TT(R(tt, n, 2 * n), Ob, w, A.mult)
        MM(i_start + [(even, mat("o"), R(tt, 0, 2 * n), False, True),
                      (R(I, e0 + 1, e0 + 2 * n, 2), mat("ohi"), R(tt, 0, n), True, True),
                      (R(I, e0 + 2 * n + 1, e0 + 4 * n, 2), mat("olo"), R(tt, n, 2 * n), True, True)])
        for k in range(2):
            SCAN(R("xj%d" % h, 2 * k * n, 2 * k * n + 2 * n), R("bz", 2 * i0, 2 * i1), at(h, "I", 2 * k, 2 * k + 2),
                 A.mult, A.add)
        lists(h, 1)
        tag[0] = "%d x%d" % (t, h)
        EITHER("gb%d" % h, gb, at(h, "D"), F.Sign, bias=col(6) + (col(10),))
        MM([(Ob, mat("um"), w, True, False), (Ob, mat("tpk"), gb, False, True)])
        EITHER("r%d" % h, r1, Ob, F.Relu, bias=col(3))
        MM([(Oc, mat("id"), w, True, False), (Oc, mat("sk"), gb, False, False), (Oc, R("imd", 0, 128), r1, False, True)])
        MM([(Od, mat("tpk"), ga, True, False), (Od, mat("ni"), w, False, True)])
        EITHER("sw%d" % h, R(sw, 512 + 2 * i0 + 1, 512 + 2 * i1, 2), Oc, bias=col(4))
        EITHER("sw%d" % h, R(sw, 512 + 2 * i0, 512 + 2 * i1, 2), Od, scale=-1.0, bias=col(7))
        cm = 128 if t == NV - 1 else 0
        MM([(Oa, mat("id"), R("cm", cm, cm + n), True, False), (Oa, mat("tpk"), ga, False, False)])

    def write_lists(t):
        tag[0] = "%d l" % t
        TS(R("sm", 0, 16), R("ui", 0, 16), 7, A.bitwise_and)
        TT(R("sm2", 0, 16), R("sm", 0, 16), R("cb", 0, 16), A.add)
        CP(R("lx", 0, 16), R("sm2", 0, 16))
        TS(R("sm", 16, 32), R("ui", 0, 16), 1, A.bitwise_and)

    def write_stock(t, i0, i1):
        c0, c1 = i0 // 16, i1 // 16
        tag[0] = "%d z" % t
        TT(R3("hh", c0, c1, 1), R("gd", c0, c1), R("sm", 16 + c0, 16 + c1), A.mult)
        TT(R3("hh", c0, c1, 0), R("gd", c0, c1), R3("hh", c0, c1, 1), A.subtract)
        TT(R3("hh", c0, c1), R3("hh", c0, c1), R3("sx", c0, c1), A.mult)
        TT(R3("hh", c0, c1), R3("hh", c0, c1), R3("sc", c0, c1), A.add)
        CP(R3("ls", c0, c1), R3("hh", c0, c1))
        for s in range(2):
            src = ind(R("sw%d" % (t % 2), 0, 512 + 2 * i1), R3("ls", c0, c1, s))
            if t < NV - 1:
                ACT(R("sw%d" % ((t + 1) % 2), 2 * i0 + s, 2 * i1, 2), src, F.Copy)
            else:
                ACT(R("op", 2 * i0 + s, 2 * i1, 2), src, bias=2048.0)
        if t == NV - 1:
            turned("op", "yp", i0, i1, 2, 4, True)

    def write_records(t, h):
        i0, i1, n, c0, c1 = sizes(h)
        y, lk, hf, av = "x%d" % ((t + 1) % 2), R("lk", c0, c1), R("hf", i0, i1), R("av", i0, i1)
        tag[0] = "%d r%d" % (t, h)
        EITHER("hf%d" % h, hf, ind(R("db%d" % h, 0, 16 * n), lk), bias=-0.25, scale=0.5)
        TT(av, ind(R("fb%d" % h, 0, 16 * n), lk), hf, A.add)
        CP(ind(R(y, 16 + 8 * i0, 16 + 8 * i1), R("lx", c0, c1)), av)
        if t == NV - 1:
            DMA(R("yx", 8 * i0, 8 * i1), R(y, 16 + 8 * i0, 16 + 8 * i1), 2)
        elif i0 == 0:
            ACT(R(y, 2064, 2096), R(y, 16, 48), F.Copy)

    def ending(t, h):
        i0, i1, n, c0, c1 = sizes(h)
        sw, O = "sw%d" % (t % 2), at(h, "O")
        gd, bj, rest, new = R("gd", c0, c1), R("bj", i0, i1), R("wz", i0, i1), R(sw, 512 + 2 * i0, 512 + 2 * i1, 2)
        tag[0] = "%d e%d" % (t, h)
        pick(h, 1)
        TT(gd, R("rs", i0 + 15, i1, 16), R("th", c0, c1), A.is_lt)
        if h == NH - 1 and t < NV - 1:
            cnt = R("ps%d" % COUNT, 0, 17)
            MM([(cnt, one, R("gd", 0, 17), True, True)])
            op("v", (64, "g", 0), [cnt], [an], lambda e: e.tensor_reduce(an[0], cnt[0], X.X, A.add, negate=True))
            TS(aq, an, M5, A.add, -M5 - 32, A.add)
        TS(at(h, "K"), at(h, "S"), col(8), A.is_equal)
        TT(bj, at(h, "K"), R("bz", 2 * i0 + 1, 2 * i1, 2), A.mult)
        MM([(R(O[1], O[2] + m, O[3], 16), R("rm", 128 * m, 128 * m + 128), gd, False, False) for m in range(16)])
        MM([(O, mat("o"), bj, False, True)])
        TT(R("g7", c0, c1), R("t2", c0, c1), gd, A.subtract)
        CP(R("lg", c0, c1), R("g7", c0, c1))
        EITHER("wz%d" % h, rest, ind(R(sw, 512 + 2 * i0, 512 + 2 * i1), R("lg", c0, c1)),
               bias=2048.0 if t == NV - 1 else 0.0)
        arr = "arr%d%d" % (t, h)
        if t < NV - 1:
            src, land = R("wo", 256 * t + i0, 256 * t + i1), R("w16", 256 * (t + 1) + i0, 256 * (t + 1) + i1)
            TT(src, O, rest, A.max)
            TT(new, O, rest, A.max)
            if rel is None:
                to, there, rs, eng = nxt, land, arr, topo.engines(core, nxt)
            else:
                to, there, rs, eng = rel, src, "hop%d%d" % (t, h), topo.engines(core, rel)
        else:
            src, land = R("wf", i0, i1), R("lf", i0, i1)
            TT(src, O, rest, A.max)
            ACT(new, src, bias=-2048.0)
            to, there, rs, eng = home, land, arr, eng_far
        rid, pid = topo.addr(to, core)
        gone = (None, "gone%d%d" % (t, h), 0, 1, 1, None)
        op("r", (200, "g", 0), [src], [gone],
           lambda e: e.remote_dma(there[0], src[0], T.sem[rs], T.sem.sent, pid, rid, mask_of(eng)), len(eng))
        way = PAR["far"] * (1 if t < NV - 1 else 0.55) + (PAR["first"] if t == 0 and h == 0 else 0)
        op("n", (way, "g", 0), [gone], [land], None, (arr, len(eng_far)))
        if t == NV - 1:
            turned("lf", "yw", i0, i1, 1, 4, True)
            write_stock(t, i0, i1)

    for t in range(NV):
        for h in range(NH):
            stage1(t, h)
        tag[0] = "%d copy" % t
        DMA(R("x%d" % ((t + 1) % 2), 16, 2064), R("x%d" % (t % 2), 16, 2064) if t else R("xt", 0, 2048), 2,
            R("off%d" % (NH - 1), 0, 2))
        for h in range(NH):
            middle(t, h)
        write_lists(t)
        for h in range(NH):
            gathers(t, 1, h)
            ending(t, h)
            write_records(t, h)
        for a, b in STOCK if t < NV - 1 else []:
            write_stock(t, a, b)
    return ops


QUEUE = {"v": "v", "s": "s", "p": "p", "g": "g", "r": "g", "y": "y", "n": "n"}


def needs(ops):
    n = len(ops)
    deps, soft = [set() for _ in range(n)], [set() for _ in range(n)]
    seen, bk = {}, {}
    for i, o in enumerate(ops):
        banks = set()
        for acc, write in ((o[2], False), (o[3], True)):
            for name, a, b in acc:
                if name in SCRATCH and SCRATCH[name][0] == "psum":
                    banks.add(name)
                for a2, b2, j, w2 in seen.get(name, []):
                    if a < b2 and a2 < b and (write or w2) and not o[0] == ops[j][0] == "p":
                        deps[i].add(j)
        for name, a, b in o[3]:
            seen[name] = [z for z in seen.get(name, []) if not (a <= z[0] and z[1] <= b)] + [(a, b, i, True)]
        for name, a, b in o[2]:
            seen.setdefault(name, []).append((a, b, i, False))
        for bank in banks:
            run, before = bk.get(bank, ([], []))
            if run and ops[run[0]][0] == o[0]:
                soft[i].add(run[-1])
                deps[i].update(before)
                run.append(i)
            else:
                deps[i].update(run)
                bk[bank] = ([i], run)
        deps[i].discard(i)
    return deps, soft


def turned_round(fore):
    back = [[] for _ in fore]
    for i, before in enumerate(fore):
        for j, gap in before:
            back[j].append((i, gap))
    return back


def first_order(ops, cost, hold, fore):
    n = len(ops)
    fore = [list(x) for x in fore]
    steps = {}
    for i, o in enumerate(ops):
        if o[6][2:3] == "g" and o[0] in LONG:
            steps.setdefault((o[6][0], o[0], o[3][0][0][0] + o[6][3:]), []).append(i)
    for q in LONG:
        row = [steps[str(t), q, name].pop(0) for t in range(NV) for name in LONG[q].split()]
        for j, i in zip(row, row[1:]):
            fore[i].append((j, 0.0))
    back = turned_round(fore)
    left = [len(x) for x in fore]
    seq = [i for i in range(n) if not left[i]]
    for i in seq:
        for j, gap in back[i]:
            left[j] -= 1
            if not left[j]:
                seq.append(j)
    chain = [0.0] * n
    for i in reversed(seq):
        chain[i] = cost[i] + max([chain[j] + gap for j, gap in back[i]] + [0.0])
    left = [len(x) for x in fore]
    free = {q: 0.0 for q in QUEUE.values()}
    ready = {q: [i for i in range(n) if not left[i] and QUEUE[ops[i][0]] == q] for q in free}
    at, start = [0.0] * n, [0.0] * n
    for _ in range(n):
        t0, q = min((max(min(at[i] for i in row), free[q]), q) for q, row in ready.items() if row)
        i = min((j for j in ready[q] if at[j] <= t0), key=lambda j: (-chain[j], j))
        soon = [j for j in ready[q] if t0 < at[j] < t0 + min(300.0, 0.35 * hold[i]) and chain[j] > chain[i]]
        if soon:
            i = min(soon, key=lambda j: (-chain[j], j))
        ready[q].remove(i)
        start[i] = max(t0, at[i])
        free[q] = start[i] + hold[i]
        for j, gap in back[i]:
            at[j] = max(at[j], start[i] + cost[i] + gap)
            left[j] -= 1
            if not left[j]:
                ready[QUEUE[ops[j][0]]].append(j)
    return sorted(range(n), key=lambda i: (start[i], i))


def survey(order, queue, cost, hold, fore, back):
    n, nq = len(order), max(queue) + 1
    end, why, before = [0.0] * n, [None] * n, []
    free, last = [0.0] * nq, [None] * nq
    for i in order:
        before.append(tuple(free))
        q = queue[i]
        t, w = free[q], (last[q], True)
        for j, gap in fore[i]:
            if end[j] + gap >= t:
                t, w = end[j] + gap, (j, False)
        end[i], free[q], last[q], why[i] = t + cost[i], t + hold[i], i, w
    top = max(end)
    i, pairs = end.index(top), []
    while why[i][0] is not None:
        if why[i][1]:
            pairs.append((why[i][0], i))
        i = why[i][0]
    rest, after, ahead = [0.0] * n, [None] * n, [0.0] * nq
    for k in range(n - 1, -1, -1):
        after[k] = tuple(ahead)
        i = order[k]
        t = max(cost[i], hold[i] + ahead[queue[i]])
        for j, gap in back[i]:
            if cost[i] + gap + rest[j] > t:
                t = cost[i] + gap + rest[j]
        rest[i] = ahead[queue[i]] = t
    return top, end, before, pairs, rest, after


def plan(ops):
    n = len(ops)
    deps, soft = needs(ops)
    queue = ["vspgyn".index(QUEUE[o[0]]) for o in ops]
    cost = [(o[1][0] + PAR[o[1][1]] * o[1][2]) * (PAR["slow"] if o[0] in "vspg" else 1) for o in ops]
    hold = [max(60.0, c - PAR["dma"]) if o[0] == "y" else 0.0 if o[0] == "n" else c for o, c in zip(ops, cost)]
    fore, reach = [], []
    for i in range(n):
        near, seen = [], 0
        for j in sorted(deps[i] | soft[i], reverse=True):
            if not seen >> j & 1:
                near.append((j, PAR["lat"] if j in deps[i] else 0.0))
            seen |= reach[j] | 1 << j
        fore.append(near)
        reach.append(seen)
    back = turned_round(fore)
    state = [PAR["seed"]]

    def draw(k):
        state[0] = (state[0] * 1103515245 + 12345) % 2 ** 31
        return (state[0] >> 8) % k

    def settle(order):
        end = survey(order, queue, cost, hold, fore, back)[1]
        order = sorted(order, key=lambda i: end[i] - cost[i])
        pos = [0] * n
        for k, i in enumerate(order):
            pos[i] = k
        return (order, pos) + survey(order, queue, cost, hold, fore, back)

    order, pos, top, end, before, pairs, rest, after = settle(first_order(ops, cost, hold, fore))
    best = (top, order)
    for it in range(PAR["tries"]):
        j, i = pairs[draw(len(pairs))]
        ahead = draw(2) == 1
        lo, hi = pos[j], pos[i]
        for _ in range(draw(4) - 1):
            k = lo - 1 if ahead else hi + 1
            while 0 <= k < n and queue[order[k]] != queue[i]:
                k += -1 if ahead else 1
            if 0 <= k < n:
                lo, hi = (k, hi) if ahead else (lo, k)
        move, todo = set(), [order[hi] if ahead else order[lo]]
        while todo:
            x = todo.pop()
            if x not in move and lo <= pos[x] <= hi:
                move.add(x)
                todo.extend(y for y, gap in (fore if ahead else back)[x])
        if order[lo if ahead else hi] in move:
            continue
        part = order[lo:hi + 1]
        part = [x for x in part if (x in move) == ahead] + [x for x in part if (x in move) != ahead]
        free, new, guess = list(before[lo]), {}, 0.0
        for x in part:
            t = max([free[queue[x]]] + [new.get(y, end[y]) + gap for y, gap in fore[x]])
            new[x], free[queue[x]] = t + cost[x], t + hold[x]
            guess = max([guess] + [new[x] + gap + rest[y] for y, gap in back[x] if pos[y] > hi])
        guess = max([guess] + [a + b for a, b in zip(free, after[hi])])
        if guess <= top + PAR["warm"] * 0.1 ** (it / PAR["tries"]) * -math.log((draw(1000) + 1) / 1001.0):
            order, pos, top, end, before, pairs, rest, after = settle(order[:lo] + part + order[hi + 1:])
            if top < best[0]:
                best = (top, order)
    return best[1], deps, best[0]


def rank_program(g, core, T, topo):
    N = len(T.cores)
    if T.rank_of(core) is None:
        for r in range(N):
            src, dst = T.cores[r], T.cores[(r + 1) % N]
            if relay_of(src, dst, topo) == core:
                relay_program(g, core, T, topo, src, dst)
        return
    ops = build(core, T, topo)
    if "order" not in PLAN:
        PLAN["order"] = plan(ops)
    order, deps = PLAN["order"][0:2]
    eng = {"v": g.vector, "s": g.scalar, "p": g.tensor, "g": g, "r": g, "y": g.sync}
    count = {"v": 0, "s": 0, "p": 0, "g": 0}
    done = {}
    seen = {q: {} for q in "vspgy"}
    sent = 0
    for i in order:
        e, c, r, w, fn, sem, name = ops[i]
        if e == "n":
            done[i] = sem
            continue
        need = {}
        for j in deps[i]:
            s, v = done[j]
            need[s] = max(need.get(s, 0), v)
        for s in sorted(need):
            if seen[QUEUE[e]].get(s, 0) < need[s]:
                eng[e].wait_ge(T.sem[s], need[s])
                seen[QUEUE[e]][s] = need[s]
        out = fn(eng[e])
        if e == "r":
            sent += sem
            done[i] = ("sent", sent)
        elif e == "y":
            out.then_inc(T.sem[sem], 16)
            done[i] = (sem, 16)
        else:
            for ins in (out if e == "p" else [out]):
                ins.then_inc(T.sem["c" + e], 1)
                count[e] += 1
            done[i] = ("c" + e, count[e])
    g.wait_ge(T.sem.sent, sent)
    last = {}
    for i in order:
        s, v = done[i]
        if s != "sent":
            last[s] = max(last.get(s, 0), v)
    for s in sorted(last):
        if seen["y"].get(s, 0) < last[s]:
            g.sync.wait_ge(T.sem[s], last[s])
